import numpy as np
import ml_dtypes


def mxq(x, axis, fmt="e4m3"):
    dtype, down = {"e4m3": (ml_dtypes.float8_e4m3fn, 7), "e5m2": (ml_dtypes.float8_e5m2, 14)}[fmt]
    v = np.moveaxis(np.asarray(x, np.float32).astype(ml_dtypes.bfloat16).astype(np.float64), axis, -1)
    blocks = v.reshape(v.shape[:-1] + (-1, 32))
    amax = np.abs(blocks).max(-1, keepdims=True)
    byte = np.maximum(np.where(amax > 0, np.frexp(amax)[1] - 1 + 127, 0) - down, 1)
    scale = np.exp2(byte - 127.0)
    codes = (blocks / scale).astype(np.float32).astype(dtype).astype(np.float64)
    return np.moveaxis((codes * scale).reshape(v.shape), -1, axis)


WIDE = False


def mx_kscale(k):
    if not WIDE:
        return np.ones(k)
    levels = np.array([18, -18])
    if k % 512:
        return np.exp2(np.random.permutation(np.resize(levels, k // 32))).repeat(32)
    a = np.empty((k // 512, 16))
    for p in range(k // 512):
        a[p, :8] = np.random.permutation(np.resize(levels, 8))
        for g in range(8):
            far = levels[np.abs(levels - a[p, g]) >= 10]
            a[p, g + 8] = far[np.random.randint(len(far))]
    return np.exp2(a.ravel()).repeat(32)


def f64(x):
    return np.asarray(x).astype(np.float64)


def striped(idx):
    return np.tile(np.asarray(idx).reshape(-1, 16).T, (8, 1)).astype(np.uint16)


def unstriped(offs):
    return offs[:16].T.reshape(-1).astype(np.int64)


B, N, T, D, R = 1, 512, 2048, 512, 512


def setup_inputs():
    n = np.random.standard_normal
    idx = np.random.permutation(T)[:B * N]
    s = mx_kscale(D)[:, None]
    z = mx_kscale(R)[:, None]
    x = n((B, D, R))
    return {
        "xT": (x * s).astype(np.float32),
        "wT": (n((D, T)) * (1.00 / np.sqrt(D)) / s).astype(np.float32),
        "y": n((B, R, N)).astype(np.float32),
        "wt": (np.random.uniform(0.5, 1.5, (B, R, 1)) * 1.0 / np.sqrt(R) * z).astype(np.float32),
        "kb": np.tile(0.5 * n(T), (128, 1)).astype(np.float32),
        "xm": (x.transpose(0, 2, 1) / z).astype(np.float32),
        "offs": striped(idx),
    }


def reference(xT, wT, y, wt, kb, xm, offs):
    idx = unstriped(offs)
    pick = lambda x: x[:, idx].reshape(x.shape[0], B, N).transpose(1, 0, 2)
    a = mxq(f64(xT), 1, "e4m3").transpose(0, 2, 1) @ mxq(pick(f64(wT)), 1, "e4m3")
    a = a + pick(f64(kb))[:, :1, :]
    g = f64(wt) * (a - f64(y))
    dw = mxq(f64(xm), 1, "e4m3").transpose(0, 2, 1) @ mxq(g, 1, "e5m2")
    gw = np.zeros((D, T))
    gw[:, idx] = dw.transpose(1, 0, 2).reshape(D, B * N)
    return gw

@@ -1,0 +1,205 @@
+from contextlib import ExitStack
+
+import concourse.mybir as mybir
+from concourse.masks import make_identity
+
+D, R, N, T = 512, 512, 512, 2048
+FLOPS = 2 * (2 * D * R * N)
+
+F32 = mybir.dt.float32
+BF16 = mybir.dt.bfloat16
+U32 = mybir.dt.uint32
+U16 = mybir.dt.uint16
+U8 = mybir.dt.uint8
+E4M3X4 = mybir.dt.float8_e4m3fn_x4
+E5M2X4 = mybir.dt.float8_e5m2_x4
+COPY = mybir.ActivationFunctionType.Copy
+MULT = mybir.AluOpType.mult
+SUBTRACT = mybir.AluOpType.subtract
+
+P = 128
+PACK = 4
+HALVES = 2
+HALF = N // HALVES
+WINDOWS = 3
+
+
+def tile_attend_gsq_w_kb_kernel(tc, xT, wT, y, wt, kb, xm, offs, out):
+    nc = tc.nc
+
+    with ExitStack() as ctx:
+        keep = ctx.enter_context(tc.tile_pool(name="keep", bufs=1))
+        psum = ctx.enter_context(tc.psum_pool(name="psum", bufs=8))
+
+        def quantize(codes, scales, grouped, dtype):
+            nc.vector.quantize_mx(out=codes.bitcast(dtype), scales=scales, in_=grouped)
+
+        offsets = keep.tile([P, N // 16], U16, name="offsets")
+        nc.sync.dma_start(offsets[:], offs)
+        row_weight = keep.tile([P, PACK], F32, name="row_weight")
+        nc.sync.dma_start(row_weight[:], wt[0].rearrange("(p j) o -> p (j o)", j=PACK))
+
+        kb_columns = keep.tile([P, T // P], F32, name="kb_columns")
+        nc.sync.dma_start(kb_columns[:], kb[0].rearrange("(p c) -> p c", p=P))
+
+        w_planes = wT.rearrange("(p j) t -> p j t", j=PACK)
+        w_raw = []
+        for j in range(PACK):
+            plane = keep.tile([P, T], F32, name="w_raw%d" % j)
+            nc.sync.dma_start(plane[:], w_planes[:, j, :])
+            w_raw.append(plane)
+
+        x_planes = xT[0].rearrange("(p j) r -> p j r", j=PACK)
+        x_raw = []
+        for h in range(HALVES):
+            part = keep.tile([P, PACK, R // HALVES], F32, name="x_raw%d" % h)
+            nc.sync.dma_start(part[:], x_planes[:, :, h * (R // HALVES) : (h + 1) * (R // HALVES)])
+            x_raw.append(part)
+
+        y_planes = y[0].rearrange("(p j) n -> p j n", j=PACK)
+        y_raw = []
+        for j in range(PACK):
+            plane = keep.tile([P, N], F32, name="y_raw%d" % j)
+            nc.sync.dma_start(plane[:], y_planes[:, j, :])
+            y_raw.append(plane)
+
+        xm_raw = keep.tile([P, PACK, D], F32, name="xm_raw")
+        nc.sync.dma_start(xm_raw[:], xm[0].rearrange("(p j) d -> p j d", j=PACK))
+
+        windows = []
+        for w in range(WINDOWS - 1):
+            window = keep.tile([P, T], F32, name="window%d" % w)
+            nc.vector.memset(window[:], 0.0)
+            windows.append(window)
+
+        identity = keep.tile([P, P], F32, name="identity")
+        make_identity(nc, identity[:])
+
+        w_grouped = keep.tile([P, N, PACK], BF16, name="w_grouped", align_bytes=64)
+
+        def gather_w(j, first, count):
+            nc.vector.tensor_copy(
+                w_grouped[:, first : first + count, j],
+                w_raw[j][:].indirect(offsets[:, first // 16 : (first + count) // 16]),
+            )
+
+        kb_window = keep.tile([P, T], F32, name="kb_window")
+        kb_items = kb_window[:].rearrange("p (n c) -> p n c", n=P)
+        for c0 in range(0, T // P, PACK):
+            spread = psum.tile([P, PACK, P], F32, name="spread", tag="bank")
+            for c in range(PACK):
+                column = kb_columns[:, c0 + c : c0 + c + 1]
+                nc.tensor.transpose(spread[:, c, :], column.to_broadcast([P, P]), identity[:])
+            nc.scalar.copy(kb_items[:, :, c0 : c0 + PACK], spread[:].rearrange("p c n -> p n c"))
+
+        gather_w(0, 0, N)
+        gather_w(1, 0, N)
+        kb_listed = keep.tile([P, N], F32, name="kb_listed")
+        nc.vector.tensor_copy(kb_listed[:], kb_window[:].indirect(offsets[:]))
+        kb_weighted = keep.tile([P, PACK, N], F32, name="kb_weighted")
+        for j in range(PACK):
+            nc.scalar.activation(kb_weighted[:, j, :], kb_listed[:], COPY, scale=row_weight[:, j : j + 1])
+
+        gather_w(2, 0, N)
+        for h in range(HALVES):
+            gather_w(3, h * HALF, HALF)
+        w_codes = keep.tile([P, N], U32, name="w_codes", align_bytes=64)
+        w_scales = keep.tile([P, N], U8, name="w_scales", align_bytes=64)
+        w_flat = w_grouped[:].rearrange("p n j -> p (n j)")
+        for h in range(HALVES):
+            cols = slice(h * HALF, (h + 1) * HALF)
+            quantize(w_codes[:, cols], w_scales[:, cols], w_flat[:, h * HALF * PACK : (h + 1) * HALF * PACK], E4M3X4)
+
+        x_grouped = keep.tile([P, PACK, P, PACK], BF16, name="x_grouped", align_bytes=64)
+        m_half = P // HALVES
+        for h in range(HALVES):
+            nc.scalar.copy(
+                x_grouped[:, :, h * m_half : (h + 1) * m_half, :].rearrange("p t m j -> p m j t"),
+                x_raw[h][:].rearrange("p j (m t) -> p m j t", t=PACK),
+            )
+
+        target = keep.tile([P, PACK, N], F32, name="target", tag="late")
+
+        def weigh_target(j):
+            nc.vector.scalar_tensor_tensor(
+                target[:, j, :], y_raw[j][:], row_weight[:, j : j + 1], kb_weighted[:, j, :], MULT, SUBTRACT
+            )
+
+        weigh_target(0)
+        x_codes = keep.tile([P, R], U32, name="x_codes", align_bytes=64)
+        x_scales = keep.tile([P, R], U8, name="x_scales", align_bytes=64)
+        x_flat = x_grouped[:].rearrange("p t m j -> p (t m j)")
+        for h in range(HALVES):
+            cols = slice(h * HALF, (h + 1) * HALF)
+            quantize(x_codes[:, cols], x_scales[:, cols], x_flat[:, h * HALF * PACK : (h + 1) * HALF * PACK], E4M3X4)
+        for j in range(1, PACK):
+            weigh_target(j)
+
+        scores = []
+        for h in range(HALVES):
+            cols = slice(h * HALF, (h + 1) * HALF)
+            weighted = keep.tile([P, PACK, HALF], F32, name="scores%d" % h)
+            for t in range(PACK):
+                rows = slice(t * P, (t + 1) * P)
+                acc = psum.tile([P, HALF], F32, name="acc", tag="bank")
+                nc.tensor.matmul_mx(
+                    out=acc[:],
+                    lhsT=x_codes[:, rows].bitcast(E4M3X4),
+                    lhsT_scale=x_scales[:, rows],
+                    rhs=w_codes[:, cols].bitcast(E4M3X4),
+                    rhs_scale=w_scales[:, cols],
+                    start=True,
+                    stop=True,
+                )
+                nc.scalar.activation(weighted[:, t, :], acc[:], COPY, scale=row_weight[:, t : t + 1])
+            scores.append(weighted)
+
+        g_grouped = keep.tile([P, N, PACK], BF16, name="g_grouped", align_bytes=64)
+        g_codes = keep.tile([P, N], U32, name="g_codes", align_bytes=64)
+        g_scales = keep.tile([P, N], U8, name="g_scales", align_bytes=64)
+        g_flat = g_grouped[:].rearrange("p n j -> p (n j)")
+        for h in range(HALVES):
+            cols = slice(h * HALF, (h + 1) * HALF)
+            nc.vector.tensor_tensor(
+                g_grouped[:, cols, :].rearrange("p (c i) t -> p c t i", i=2),
+                scores[h][:].rearrange("p t (c i) -> p c t i", i=2),
+                target[:, :, cols].rearrange("p t (c i) -> p c t i", i=2),
+                SUBTRACT,
+            )
+        for h in range(HALVES):
+            cols = slice(h * HALF, (h + 1) * HALF)
+            quantize(g_codes[:, cols], g_scales[:, cols], g_flat[:, h * HALF * PACK : (h + 1) * HALF * PACK], E5M2X4)
+
+        xm_grouped = keep.tile([P, D, PACK], BF16, name="xm_grouped", align_bytes=64)
+        xm_codes = keep.tile([P, D], U32, name="xm_codes", align_bytes=64)
+        xm_scales = keep.tile([P, D], U8, name="xm_scales", align_bytes=64)
+        xm_flat = xm_grouped[:].rearrange("p d j -> p (d j)")
+        for e in range(D // P):
+            feats = slice(e * P, (e + 1) * P)
+            nc.scalar.copy(
+                xm_grouped[:, feats, :].rearrange("p (c i) j -> p c j i", i=2),
+                xm_raw[:, :, feats].rearrange("p j (c i) -> p c j i", i=2),
+            )
+            quantize(xm_codes[:, feats], xm_scales[:, feats], xm_flat[:, e * P * PACK : (e + 1) * P * PACK], E4M3X4)
+
+        last_window = keep.tile([P, T], F32, name="last_window", tag="late")
+        nc.vector.memset(last_window[:], 0.0)
+        windows.append(last_window)
+
+        for e in range(D // P):
+            feats = slice(e * P, (e + 1) * P)
+            acc = psum.tile([P, N], F32, name="acc", tag="bank")
+            nc.tensor.matmul_mx(
+                out=acc[:],
+                lhsT=xm_codes[:, feats].bitcast(E4M3X4),
+                lhsT_scale=xm_scales[:, feats],
+                rhs=g_codes[:].bitcast(E5M2X4),
+                rhs_scale=g_scales[:],
+                start=True,
+                stop=True,
+            )
+            gradient = keep.tile([P, N], F32, name="gradient%d" % e)
+            nc.scalar.copy(gradient[:], acc[:])
+            window = windows[e % WINDOWS]
+            nc.vector.tensor_copy(window[:].indirect(offsets[:]), gradient[:])
+            nc.sync.dma_start(out[feats, :], window[:])

@@ -8,6 +8,7 @@ FLOPS = 2 * (2 * D * R * N)
 
 F32 = mybir.dt.float32
 BF16 = mybir.dt.bfloat16
+I32 = mybir.dt.int32
 U32 = mybir.dt.uint32
 U16 = mybir.dt.uint16
 U8 = mybir.dt.uint8
@@ -35,9 +36,7 @@ def tile_attend_gsq_w_kb_kernel(tc, xT, wT, y, wt, kb, xm, offs, out):
             nc.vector.quantize_mx(out=codes.bitcast(dtype), scales=scales, in_=grouped)
 
         offsets = keep.tile([P, N // 16], U16, name="offsets")
-        nc.sync.dma_start(offsets[:], offs)
         row_weight = keep.tile([P, PACK], F32, name="row_weight")
-        nc.sync.dma_start(row_weight[:], wt[0].rearrange("(p j) o -> p (j o)", j=PACK))
 
         kb_columns = keep.tile([P, T // P], F32, name="kb_columns")
         nc.sync.dma_start(kb_columns[:], kb[0].rearrange("(p c) -> p c", p=P))
@@ -48,6 +47,9 @@ def tile_attend_gsq_w_kb_kernel(tc, xT, wT, y, wt, kb, xm, offs, out):
             plane = keep.tile([P, T], F32, name="w_raw%d" % j)
             nc.sync.dma_start(plane[:], w_planes[:, j, :])
             w_raw.append(plane)
+            if j == 0:
+                nc.sync.dma_start(offsets[:], offs)
+                nc.sync.dma_start(row_weight[:], wt[0].rearrange("(p j) o -> p (j o)", j=PACK))
 
         x_planes = xT[0].rearrange("(p j) r -> p j r", j=PACK)
         x_raw = []
@@ -67,23 +69,15 @@ def tile_attend_gsq_w_kb_kernel(tc, xT, wT, y, wt, kb, xm, offs, out):
         nc.sync.dma_start(xm_raw[:], xm[0].rearrange("(p j) d -> p j d", j=PACK))
 
         windows = []
-        for w in range(WINDOWS - 1):
+        for w in range(WINDOWS):
             window = keep.tile([P, T], F32, name="window%d" % w)
-            nc.vector.memset(window[:], 0.0)
+            nc.vector.memset(window[:].bitcast(I32), 0)
             windows.append(window)
 
         identity = keep.tile([P, P], F32, name="identity")
         make_identity(nc, identity[:])
 
-        w_grouped = keep.tile([P, N, PACK], BF16, name="w_grouped", align_bytes=64)
-
-        def gather_w(j, first, count):
-            nc.vector.tensor_copy(
-                w_grouped[:, first : first + count, j],
-                w_raw[j][:].indirect(offsets[:, first // 16 : (first + count) // 16]),
-            )
-
-        kb_window = keep.tile([P, T], F32, name="kb_window")
+        kb_window = keep.tile([P, T], F32, name="kb_window", tag="zeroth", align_bytes=64)
         kb_items = kb_window[:].rearrange("p (n c) -> p n c", n=P)
         for c0 in range(0, T // P, PACK):
             spread = psum.tile([P, PACK, P], F32, name="spread", tag="bank")
@@ -92,15 +86,22 @@ def tile_attend_gsq_w_kb_kernel(tc, xT, wT, y, wt, kb, xm, offs, out):
                 nc.tensor.transpose(spread[:, c, :], column.to_broadcast([P, P]), identity[:])
             nc.scalar.copy(kb_items[:, :, c0 : c0 + PACK], spread[:].rearrange("p c n -> p n c"))
 
-        gather_w(0, 0, N)
-        gather_w(1, 0, N)
-        kb_listed = keep.tile([P, N], F32, name="kb_listed")
+        kb_listed = keep.tile([P, N], F32, name="kb_listed", tag="first", align_bytes=64)
         nc.vector.tensor_copy(kb_listed[:], kb_window[:].indirect(offsets[:]))
         kb_weighted = keep.tile([P, PACK, N], F32, name="kb_weighted")
         for j in range(PACK):
             nc.scalar.activation(kb_weighted[:, j, :], kb_listed[:], COPY, scale=row_weight[:, j : j + 1])
 
-        gather_w(2, 0, N)
+        w_grouped = keep.tile([P, N, PACK], BF16, name="w_grouped", tag="zeroth", align_bytes=64)
+
+        def gather_w(j, first, count):
+            nc.vector.tensor_copy(
+                w_grouped[:, first : first + count, j],
+                w_raw[j][:].indirect(offsets[:, first // 16 : (first + count) // 16]),
+            )
+
+        for j in range(PACK - 1):
+            gather_w(j, 0, N)
         for h in range(HALVES):
             gather_w(3, h * HALF, HALF)
         w_codes = keep.tile([P, N], U32, name="w_codes", align_bytes=64)
@@ -110,29 +111,31 @@ def tile_attend_gsq_w_kb_kernel(tc, xT, wT, y, wt, kb, xm, offs, out):
             cols = slice(h * HALF, (h + 1) * HALF)
             quantize(w_codes[:, cols], w_scales[:, cols], w_flat[:, h * HALF * PACK : (h + 1) * HALF * PACK], E4M3X4)
 
-        x_grouped = keep.tile([P, PACK, P, PACK], BF16, name="x_grouped", align_bytes=64)
+        x_grouped = [
+            keep.tile([P, 2, P, PACK], BF16, name="x_grouped%d" % u, tag=tag, align_bytes=64)
+            for u, tag in enumerate(("first", "second"))
+        ]
         m_half = P // HALVES
         for h in range(HALVES):
-            nc.scalar.copy(
-                x_grouped[:, :, h * m_half : (h + 1) * m_half, :].rearrange("p t m j -> p m j t"),
-                x_raw[h][:].rearrange("p j (m t) -> p m j t", t=PACK),
-            )
+            for u in range(2):
+                nc.scalar.copy(
+                    x_grouped[u][:, :, h * m_half : (h + 1) * m_half, :].rearrange("p t m j -> p m j t"),
+                    x_raw[h][:].rearrange("p j (m t) -> p m j t", t=PACK)[:, :, :, 2 * u : 2 * u + 2],
+                )
+        x_codes = keep.tile([P, R], U32, name="x_codes", tag="third", align_bytes=64)
+        x_scales = keep.tile([P, R], U8, name="x_scales", align_bytes=64)
+        for u in range(2):
+            cols = slice(u * 2 * P, (u + 1) * 2 * P)
+            quantize(x_codes[:, cols], x_scales[:, cols], x_grouped[u][:].rearrange("p t m j -> p (t m j)"), E4M3X4)
 
-        target = keep.tile([P, PACK, N], F32, name="target", tag="late")
+        target = keep.tile([P, PACK, N], F32, name="target", tag="first", align_bytes=64)
 
         def weigh_target(j):
             nc.vector.scalar_tensor_tensor(
                 target[:, j, :], y_raw[j][:], row_weight[:, j : j + 1], kb_weighted[:, j, :], MULT, SUBTRACT
             )
 
-        weigh_target(0)
-        x_codes = keep.tile([P, R], U32, name="x_codes", align_bytes=64)
-        x_scales = keep.tile([P, R], U8, name="x_scales", align_bytes=64)
-        x_flat = x_grouped[:].rearrange("p t m j -> p (t m j)")
-        for h in range(HALVES):
-            cols = slice(h * HALF, (h + 1) * HALF)
-            quantize(x_codes[:, cols], x_scales[:, cols], x_flat[:, h * HALF * PACK : (h + 1) * HALF * PACK], E4M3X4)
-        for j in range(1, PACK):
+        for j in range(PACK):
             weigh_target(j)
 
         scores = []
@@ -170,7 +173,7 @@ def tile_attend_gsq_w_kb_kernel(tc, xT, wT, y, wt, kb, xm, offs, out):
             cols = slice(h * HALF, (h + 1) * HALF)
             quantize(g_codes[:, cols], g_scales[:, cols], g_flat[:, h * HALF * PACK : (h + 1) * HALF * PACK], E5M2X4)
 
-        xm_grouped = keep.tile([P, D, PACK], BF16, name="xm_grouped", align_bytes=64)
+        xm_grouped = keep.tile([P, D, PACK], BF16, name="xm_grouped", tag="third", align_bytes=64)
         xm_codes = keep.tile([P, D], U32, name="xm_codes", align_bytes=64)
         xm_scales = keep.tile([P, D], U8, name="xm_scales", align_bytes=64)
         xm_flat = xm_grouped[:].rearrange("p d j -> p (d j)")
@@ -181,10 +184,6 @@ def tile_attend_gsq_w_kb_kernel(tc, xT, wT, y, wt, kb, xm, offs, out):
                 xm_raw[:, :, feats].rearrange("p j (c i) -> p c j i", i=2),
             )
             quantize(xm_codes[:, feats], xm_scales[:, feats], xm_flat[:, e * P * PACK : (e + 1) * P * PACK], E4M3X4)
-
-        last_window = keep.tile([P, T], F32, name="last_window", tag="late")
-        nc.vector.memset(last_window[:], 0.0)
-        windows.append(last_window)
 
         for e in range(D // P):
             feats = slice(e * P, (e + 1) * P)

@@ -20,6 +20,8 @@ SUBTRACT = mybir.AluOpType.subtract
 
 P = 128
 PACK = 4
+BAND = 16
+BANKS = 8
 HALVES = 2
 HALF = N // HALVES
 WINDOWS = 3
@@ -27,170 +29,151 @@ WINDOWS = 3
 
 def tile_attend_gsq_w_kb_kernel(tc, xT, wT, y, wt, kb, xm, offs, out):
     nc = tc.nc
+    halves = [slice(h * HALF, (h + 1) * HALF) for h in range(HALVES)]
 
     with ExitStack() as ctx:
         keep = ctx.enter_context(tc.tile_pool(name="keep", bufs=1))
-        psum = ctx.enter_context(tc.psum_pool(name="psum", bufs=8))
+        psum = ctx.enter_context(tc.psum_pool(name="psum", bufs=BANKS))
 
         def quantize(codes, scales, grouped, dtype):
-            nc.vector.quantize_mx(out=codes.bitcast(dtype), scales=scales, in_=grouped)
+            nc.vector.quantize_mx(out=codes.bitcast(dtype), scales=scales, in_=grouped.rearrange("p c t -> p (c t)"))
 
-        offsets = keep.tile([P, N // 16], U16, name="offsets")
-        row_weight = keep.tile([P, PACK], F32, name="row_weight")
+        def group(copy, grouped, planes):
+            copy(grouped.rearrange("p (c i) t -> p c t i", i=4), planes.rearrange("p t (c i) -> p c t i", i=4))
 
         kb_columns = keep.tile([P, T // P], F32, name="kb_columns")
         nc.sync.dma_start(kb_columns[:], kb[0].rearrange("(p c) -> p c", p=P))
 
-        w_planes = wT.rearrange("(p j) t -> p j t", j=PACK)
-        w_raw = []
-        for j in range(PACK):
-            plane = keep.tile([P, T], F32, name="w_raw%d" % j)
-            nc.sync.dma_start(plane[:], w_planes[:, j, :])
-            w_raw.append(plane)
-            if j == 0:
-                nc.sync.dma_start(offsets[:], offs)
-                nc.sync.dma_start(row_weight[:], wt[0].rearrange("(p j) o -> p (j o)", j=PACK))
+        w_planes = wT.rearrange("(p t) c -> p t c", t=PACK)
+        w_raw = [keep.tile([P, T], F32, name="w_raw%d" % t) for t in range(PACK)]
+        nc.sync.dma_start(w_raw[0][:], w_planes[:, 0, :])
+        offsets = keep.tile([P, N // BAND], U16, name="offsets")
+        nc.sync.dma_start(offsets[:], offs)
+        row_weight = keep.tile([P, PACK], F32, name="row_weight")
+        nc.sync.dma_start(row_weight[:], wt[0].rearrange("(p t) o -> p (t o)", t=PACK))
+        for t in range(1, PACK):
+            nc.sync.dma_start(w_raw[t][:], w_planes[:, t, :])
 
-        x_planes = xT[0].rearrange("(p j) r -> p j r", j=PACK)
-        x_raw = []
+        x_planes = xT[0].rearrange("(p t) r -> p t r", t=PACK)
+        x_raw = [keep.tile([P, PACK, R // HALVES], F32, name="x_raw%d" % h) for h in range(HALVES)]
         for h in range(HALVES):
-            part = keep.tile([P, PACK, R // HALVES], F32, name="x_raw%d" % h)
-            nc.sync.dma_start(part[:], x_planes[:, :, h * (R // HALVES) : (h + 1) * (R // HALVES)])
-            x_raw.append(part)
+            nc.sync.dma_start(x_raw[h][:], x_planes[:, :, h * (R // HALVES) : (h + 1) * (R // HALVES)])
 
-        y_planes = y[0].rearrange("(p j) n -> p j n", j=PACK)
-        y_raw = []
-        for j in range(PACK):
-            plane = keep.tile([P, N], F32, name="y_raw%d" % j)
-            nc.sync.dma_start(plane[:], y_planes[:, j, :])
-            y_raw.append(plane)
+        y_planes = y[0].rearrange("(p t) n -> p t n", t=PACK)
+        y_raw = [keep.tile([P, N], F32, name="y_raw%d" % t) for t in range(PACK)]
+        for t in range(PACK):
+            nc.sync.dma_start(y_raw[t][:], y_planes[:, t, :])
 
         xm_raw = keep.tile([P, PACK, D], F32, name="xm_raw")
-        nc.sync.dma_start(xm_raw[:], xm[0].rearrange("(p j) d -> p j d", j=PACK))
+        nc.sync.dma_start(xm_raw[:], xm[0].rearrange("(p t) d -> p t d", t=PACK))
 
-        windows = []
-        for w in range(WINDOWS):
-            window = keep.tile([P, T], F32, name="window%d" % w)
+        windows = [keep.tile([P, T], F32, name="window%d" % w) for w in range(WINDOWS)]
+        for window in windows:
             nc.vector.memset(window[:].bitcast(I32), 0)
-            windows.append(window)
 
         identity = keep.tile([P, P], F32, name="identity")
         make_identity(nc, identity[:])
-
-        kb_window = keep.tile([P, T], F32, name="kb_window", tag="zeroth", align_bytes=64)
+        kb_window = keep.tile([P, T], F32, name="kb_window", tag="kb_then_w", align_bytes=64)
         kb_items = kb_window[:].rearrange("p (n c) -> p n c", n=P)
-        for c0 in range(0, T // P, PACK):
-            spread = psum.tile([P, PACK, P], F32, name="spread", tag="bank")
-            for c in range(PACK):
+        turns_per_bank = N // P
+        for c0 in range(0, T // P, turns_per_bank):
+            spread = psum.tile([P, turns_per_bank, P], F32, name="spread", tag="bank")
+            for c in range(turns_per_bank):
                 column = kb_columns[:, c0 + c : c0 + c + 1]
                 nc.tensor.transpose(spread[:, c, :], column.to_broadcast([P, P]), identity[:])
-            nc.scalar.copy(kb_items[:, :, c0 : c0 + PACK], spread[:].rearrange("p c n -> p n c"))
+            nc.scalar.copy(kb_items[:, :, c0 : c0 + turns_per_bank], spread[:].rearrange("p c n -> p n c"))
 
-        kb_listed = keep.tile([P, N], F32, name="kb_listed", tag="first", align_bytes=64)
+        kb_listed = keep.tile([P, N], F32, name="kb_listed", tag="kb_x_target", align_bytes=64)
         nc.vector.tensor_copy(kb_listed[:], kb_window[:].indirect(offsets[:]))
         kb_weighted = keep.tile([P, PACK, N], F32, name="kb_weighted")
-        for j in range(PACK):
-            nc.scalar.activation(kb_weighted[:, j, :], kb_listed[:], COPY, scale=row_weight[:, j : j + 1])
+        for t in range(PACK):
+            nc.scalar.activation(kb_weighted[:, t, :], kb_listed[:], COPY, scale=row_weight[:, t : t + 1])
 
-        w_grouped = keep.tile([P, N, PACK], BF16, name="w_grouped", tag="zeroth", align_bytes=64)
-
-        def gather_w(j, first, count):
-            nc.vector.tensor_copy(
-                w_grouped[:, first : first + count, j],
-                w_raw[j][:].indirect(offsets[:, first // 16 : (first + count) // 16]),
-            )
-
-        for j in range(PACK - 1):
-            gather_w(j, 0, N)
-        for h in range(HALVES):
-            gather_w(3, h * HALF, HALF)
+        w_listed = keep.tile([P, PACK, N], BF16, name="w_listed", tag="kb_then_w", align_bytes=64)
+        for t in range(PACK - 1):
+            nc.vector.tensor_copy(w_listed[:, t, :], w_raw[t][:].indirect(offsets[:]))
+        for slots in halves:
+            listed = offsets[:, slots.start // BAND : slots.stop // BAND]
+            nc.vector.tensor_copy(w_listed[:, PACK - 1, slots], w_raw[PACK - 1][:].indirect(listed))
+        w_grouped = keep.tile([P, N, PACK], BF16, name="w_grouped", align_bytes=64)
         w_codes = keep.tile([P, N], U32, name="w_codes", align_bytes=64)
         w_scales = keep.tile([P, N], U8, name="w_scales", align_bytes=64)
-        w_flat = w_grouped[:].rearrange("p n j -> p (n j)")
-        for h in range(HALVES):
-            cols = slice(h * HALF, (h + 1) * HALF)
-            quantize(w_codes[:, cols], w_scales[:, cols], w_flat[:, h * HALF * PACK : (h + 1) * HALF * PACK], E4M3X4)
+        for slots in halves:
+            group(nc.vector.tensor_copy, w_grouped[:, slots, :], w_listed[:, :, slots])
+        for slots in halves:
+            quantize(w_codes[:, slots], w_scales[:, slots], w_grouped[:, slots, :], E4M3X4)
 
         x_grouped = [
-            keep.tile([P, 2, P, PACK], BF16, name="x_grouped%d" % u, tag=tag, align_bytes=64)
-            for u, tag in enumerate(("first", "second"))
+            keep.tile([P, 2, P, PACK], BF16, name="x_grouped0", tag="kb_x_target", align_bytes=64),
+            keep.tile([P, 2, P, PACK], BF16, name="x_grouped1", align_bytes=64),
         ]
         m_half = P // HALVES
         for h in range(HALVES):
             for u in range(2):
                 nc.scalar.copy(
-                    x_grouped[u][:, :, h * m_half : (h + 1) * m_half, :].rearrange("p t m j -> p m j t"),
-                    x_raw[h][:].rearrange("p j (m t) -> p m j t", t=PACK)[:, :, :, 2 * u : 2 * u + 2],
+                    x_grouped[u][:, :, h * m_half : (h + 1) * m_half, :].rearrange("p s m t -> p m t s"),
+                    x_raw[h][:].rearrange("p t (m s) -> p m t s", s=PACK)[:, :, :, 2 * u : 2 * u + 2],
                 )
-        x_codes = keep.tile([P, R], U32, name="x_codes", tag="third", align_bytes=64)
+        x_codes = keep.tile([P, R], U32, name="x_codes", tag="x_then_xm", align_bytes=64)
         x_scales = keep.tile([P, R], U8, name="x_scales", align_bytes=64)
         for u in range(2):
             cols = slice(u * 2 * P, (u + 1) * 2 * P)
-            quantize(x_codes[:, cols], x_scales[:, cols], x_grouped[u][:].rearrange("p t m j -> p (t m j)"), E4M3X4)
+            quantize(x_codes[:, cols], x_scales[:, cols], x_grouped[u][:].rearrange("p s m t -> p (s m) t"), E4M3X4)
 
-        target = keep.tile([P, PACK, N], F32, name="target", tag="first", align_bytes=64)
+        target = keep.tile([P, PACK, N], F32, name="target", tag="kb_x_target", align_bytes=64)
 
-        def weigh_target(j):
+        def weigh_target(s, slots):
             nc.vector.scalar_tensor_tensor(
-                target[:, j, :], y_raw[j][:], row_weight[:, j : j + 1], kb_weighted[:, j, :], MULT, SUBTRACT
+                target[:, s, slots], y_raw[s][:, slots], row_weight[:, s : s + 1], kb_weighted[:, s, slots], MULT, SUBTRACT
             )
 
-        for j in range(PACK):
-            weigh_target(j)
+        for s in range(PACK - 1):
+            weigh_target(s, slice(0, N))
+        for slots in halves:
+            weigh_target(PACK - 1, slots)
 
-        scores = []
-        for h in range(HALVES):
-            cols = slice(h * HALF, (h + 1) * HALF)
-            weighted = keep.tile([P, PACK, HALF], F32, name="scores%d" % h)
-            for t in range(PACK):
-                rows = slice(t * P, (t + 1) * P)
-                acc = psum.tile([P, HALF], F32, name="acc", tag="bank")
+        scores = [keep.tile([P, PACK, HALF], F32, name="scores%d" % h) for h in range(HALVES)]
+        for h, slots in enumerate(halves):
+            for s in range(PACK):
+                rows = slice(s * P, (s + 1) * P)
+                score_bank = psum.tile([P, HALF], F32, name="score_bank", tag="bank")
                 nc.tensor.matmul_mx(
-                    out=acc[:],
+                    out=score_bank[:],
                     lhsT=x_codes[:, rows].bitcast(E4M3X4),
                     lhsT_scale=x_scales[:, rows],
-                    rhs=w_codes[:, cols].bitcast(E4M3X4),
-                    rhs_scale=w_scales[:, cols],
+                    rhs=w_codes[:, slots].bitcast(E4M3X4),
+                    rhs_scale=w_scales[:, slots],
                     start=True,
                     stop=True,
                 )
-                nc.scalar.activation(weighted[:, t, :], acc[:], COPY, scale=row_weight[:, t : t + 1])
-            scores.append(weighted)
+                nc.scalar.activation(scores[h][:, s, :], score_bank[:], COPY, scale=row_weight[:, s : s + 1])
 
         g_grouped = keep.tile([P, N, PACK], BF16, name="g_grouped", align_bytes=64)
         g_codes = keep.tile([P, N], U32, name="g_codes", align_bytes=64)
         g_scales = keep.tile([P, N], U8, name="g_scales", align_bytes=64)
-        g_flat = g_grouped[:].rearrange("p n j -> p (n j)")
-        for h in range(HALVES):
-            cols = slice(h * HALF, (h + 1) * HALF)
+        for h, slots in enumerate(halves):
             nc.vector.tensor_tensor(
-                g_grouped[:, cols, :].rearrange("p (c i) t -> p c t i", i=2),
-                scores[h][:].rearrange("p t (c i) -> p c t i", i=2),
-                target[:, :, cols].rearrange("p t (c i) -> p c t i", i=2),
+                g_grouped[:, slots, :].rearrange("p (c i) s -> p c s i", i=2),
+                scores[h][:].rearrange("p s (c i) -> p c s i", i=2),
+                target[:, :, slots].rearrange("p s (c i) -> p c s i", i=2),
                 SUBTRACT,
             )
-        for h in range(HALVES):
-            cols = slice(h * HALF, (h + 1) * HALF)
-            quantize(g_codes[:, cols], g_scales[:, cols], g_flat[:, h * HALF * PACK : (h + 1) * HALF * PACK], E5M2X4)
+        for slots in halves:
+            quantize(g_codes[:, slots], g_scales[:, slots], g_grouped[:, slots, :], E5M2X4)
 
-        xm_grouped = keep.tile([P, D, PACK], BF16, name="xm_grouped", tag="third", align_bytes=64)
-        xm_codes = keep.tile([P, D], U32, name="xm_codes", align_bytes=64)
         xm_scales = keep.tile([P, D], U8, name="xm_scales", align_bytes=64)
-        xm_flat = xm_grouped[:].rearrange("p d j -> p (d j)")
-        for e in range(D // P):
-            feats = slice(e * P, (e + 1) * P)
-            nc.scalar.copy(
-                xm_grouped[:, feats, :].rearrange("p (c i) j -> p c j i", i=2),
-                xm_raw[:, :, feats].rearrange("p j (c i) -> p c j i", i=2),
-            )
-            quantize(xm_codes[:, feats], xm_scales[:, feats], xm_flat[:, e * P * PACK : (e + 1) * P * PACK], E4M3X4)
 
-        for e in range(D // P):
+        def quantize_xm(e, grouped, codes):
             feats = slice(e * P, (e + 1) * P)
-            acc = psum.tile([P, N], F32, name="acc", tag="bank")
+            group(nc.scalar.copy, grouped, xm_raw[:, :, feats])
+            quantize(codes, xm_scales[:, feats], grouped, E4M3X4)
+
+        def scatter_gradient(e, codes):
+            feats = slice(e * P, (e + 1) * P)
+            gradient_bank = psum.tile([P, N], F32, name="gradient_bank", tag="bank")
             nc.tensor.matmul_mx(
-                out=acc[:],
-                lhsT=xm_codes[:, feats].bitcast(E4M3X4),
+                out=gradient_bank[:],
+                lhsT=codes.bitcast(E4M3X4),
                 lhsT_scale=xm_scales[:, feats],
                 rhs=g_codes[:].bitcast(E5M2X4),
                 rhs_scale=g_scales[:],
@@ -198,7 +181,20 @@ def tile_attend_gsq_w_kb_kernel(tc, xT, wT, y, wt, kb, xm, offs, out):
                 stop=True,
             )
             gradient = keep.tile([P, N], F32, name="gradient%d" % e)
-            nc.scalar.copy(gradient[:], acc[:])
+            nc.scalar.copy(gradient[:], gradient_bank[:])
             window = windows[e % WINDOWS]
             nc.vector.tensor_copy(window[:].indirect(offsets[:]), gradient[:])
             nc.sync.dma_start(out[feats, :], window[:])
+
+        last = D // P - 1
+        xm_grouped = keep.tile([P, last * P, PACK], BF16, name="xm_grouped", tag="x_then_xm", align_bytes=64)
+        first_codes = keep.tile([P, P], U32, name="first_codes", tag="first_then_last", align_bytes=64)
+        later_codes = keep.tile([P, last * P], U32, name="later_codes", align_bytes=64)
+        xm_codes = [first_codes[:]] + [later_codes[:, k * P : (k + 1) * P] for k in range(last)]
+        for e in range(last):
+            quantize_xm(e, xm_grouped[:, e * P : (e + 1) * P, :], xm_codes[e])
+        scatter_gradient(0, xm_codes[0])
+        last_grouped = keep.tile([P, P, PACK], BF16, name="last_grouped", tag="first_then_last", align_bytes=64)
+        quantize_xm(last, last_grouped[:], xm_codes[last])
+        for e in range(1, last + 1):
+            scatter_gradient(e, xm_codes[e])

@@ -33,6 +33,7 @@ def tile_attend_gsq_w_kb_kernel(tc, xT, wT, y, wt, kb, xm, offs, out):
 
     with ExitStack() as ctx:
         keep = ctx.enter_context(tc.tile_pool(name="keep", bufs=1))
+        shared = ctx.enter_context(tc.tile_pool(name="shared", bufs=1))
         psum = ctx.enter_context(tc.psum_pool(name="psum", bufs=BANKS))
 
         def quantize(codes, scales, grouped, dtype):
@@ -60,20 +61,20 @@ def tile_attend_gsq_w_kb_kernel(tc, xT, wT, y, wt, kb, xm, offs, out):
             nc.sync.dma_start(x_raw[h][:], x_planes[:, :, h * (R // HALVES) : (h + 1) * (R // HALVES)])
 
         y_planes = y[0].rearrange("(p t) n -> p t n", t=PACK)
-        y_raw = [keep.tile([P, N], F32, name="y_raw%d" % t) for t in range(PACK)]
-        for t in range(PACK):
-            nc.sync.dma_start(y_raw[t][:], y_planes[:, t, :])
+        y_pairs = [keep.tile([P, 2, N], F32, name="y_pair%d" % u) for u in range(2)]
+        for u in range(2):
+            nc.sync.dma_start(y_pairs[u][:], y_planes[:, 2 * u : 2 * u + 2, :])
+        y_raw = [y_pairs[t // 2][:, t % 2, :] for t in range(PACK)]
 
         xm_raw = keep.tile([P, PACK, D], F32, name="xm_raw")
         nc.sync.dma_start(xm_raw[:], xm[0].rearrange("(p t) d -> p t d", t=PACK))
 
-        windows = [keep.tile([P, T], F32, name="window%d" % w) for w in range(WINDOWS)]
+        identity = keep.tile([P, P], F32, name="identity", tag="identity_then_window")
+        make_identity(nc, identity[:])
+        windows = [keep.tile([P, T], F32, name="window%d" % w) for w in range(WINDOWS - 1)]
         for window in windows:
             nc.vector.memset(window[:].bitcast(I32), 0)
-
-        identity = keep.tile([P, P], F32, name="identity")
-        make_identity(nc, identity[:])
-        kb_window = keep.tile([P, T], F32, name="kb_window", tag="kb_then_w", align_bytes=64)
+        kb_window = shared.tile([P, T], F32, name="kb_window", offset=0, align_bytes=64)
         kb_items = kb_window[:].rearrange("p (n c) -> p n c", n=P)
         turns_per_bank = N // P
         for c0 in range(0, T // P, turns_per_bank):
@@ -83,25 +84,40 @@ def tile_attend_gsq_w_kb_kernel(tc, xT, wT, y, wt, kb, xm, offs, out):
                 nc.tensor.transpose(spread[:, c, :], column.to_broadcast([P, P]), identity[:])
             nc.scalar.copy(kb_items[:, :, c0 : c0 + turns_per_bank], spread[:].rearrange("p c n -> p n c"))
 
+        windows.append(keep.tile([P, T], F32, name="last_window", tag="identity_then_window"))
+        nc.gpsimd.memset(windows[-1][:].bitcast(I32), 0)
+
         kb_listed = keep.tile([P, N], F32, name="kb_listed", tag="kb_x_target", align_bytes=64)
         nc.vector.tensor_copy(kb_listed[:], kb_window[:].indirect(offsets[:]))
         kb_weighted = keep.tile([P, PACK, N], F32, name="kb_weighted")
         for t in range(PACK):
             nc.scalar.activation(kb_weighted[:, t, :], kb_listed[:], COPY, scale=row_weight[:, t : t + 1])
 
-        w_listed = keep.tile([P, PACK, N], BF16, name="w_listed", tag="kb_then_w", align_bytes=64)
+        w_listed = [
+            shared.tile([P, 2, N], BF16, name="w_listed0", offset=6144, align_bytes=64),
+            shared.tile([P, 2, N], BF16, name="w_listed1", offset=0, align_bytes=64),
+        ]
+        w_grouped = [
+            shared.tile([P, HALF, PACK], BF16, name="w_grouped%d" % h, offset=2048 * (h + 1), align_bytes=64)
+            for h in range(HALVES)
+        ]
+
+        def group_pair(copy, u, h):
+            copy(w_grouped[h][:, :, 2 * u : 2 * u + 2], w_listed[u][:, :, halves[h]].rearrange("p t c -> p c t"))
+
         for t in range(PACK - 1):
-            nc.vector.tensor_copy(w_listed[:, t, :], w_raw[t][:].indirect(offsets[:]))
-        for slots in halves:
+            nc.vector.tensor_copy(w_listed[t // 2][:, t % 2, :], w_raw[t][:].indirect(offsets[:]))
+        for h in range(HALVES):
+            group_pair(nc.scalar.copy, 0, h)
+        for slots in reversed(halves):
             listed = offsets[:, slots.start // BAND : slots.stop // BAND]
-            nc.vector.tensor_copy(w_listed[:, PACK - 1, slots], w_raw[PACK - 1][:].indirect(listed))
-        w_grouped = keep.tile([P, N, PACK], BF16, name="w_grouped", align_bytes=64)
+            nc.vector.tensor_copy(w_listed[1][:, 1, slots], w_raw[PACK - 1][:].indirect(listed))
         w_codes = keep.tile([P, N], U32, name="w_codes", align_bytes=64)
         w_scales = keep.tile([P, N], U8, name="w_scales", align_bytes=64)
-        for slots in halves:
-            group(nc.vector.tensor_copy, w_grouped[:, slots, :], w_listed[:, :, slots])
-        for slots in halves:
-            quantize(w_codes[:, slots], w_scales[:, slots], w_grouped[:, slots, :], E4M3X4)
+        group_pair(nc.scalar.copy, 1, 1)
+        group_pair(nc.vector.tensor_copy, 1, 0)
+        for h, slots in enumerate(halves):
+            quantize(w_codes[:, slots], w_scales[:, slots], w_grouped[h][:], E4M3X4)
 
         x_grouped = [
             keep.tile([P, 2, P, PACK], BF16, name="x_grouped0", tag="kb_x_target", align_bytes=64),
@@ -110,7 +126,8 @@ def tile_attend_gsq_w_kb_kernel(tc, xT, wT, y, wt, kb, xm, offs, out):
         m_half = P // HALVES
         for h in range(HALVES):
             for u in range(2):
-                nc.scalar.copy(
+                copy = nc.vector.tensor_copy if (h, u) == (1, 0) else nc.scalar.copy
+                copy(
                     x_grouped[u][:, :, h * m_half : (h + 1) * m_half, :].rearrange("p s m t -> p m t s"),
                     x_raw[h][:].rearrange("p t (m s) -> p m t s", s=PACK)[:, :, :, 2 * u : 2 * u + 2],
                 )
@@ -148,53 +165,67 @@ def tile_attend_gsq_w_kb_kernel(tc, xT, wT, y, wt, kb, xm, offs, out):
                 )
                 nc.scalar.activation(scores[h][:, s, :], score_bank[:], COPY, scale=row_weight[:, s : s + 1])
 
-        g_grouped = keep.tile([P, N, PACK], BF16, name="g_grouped", align_bytes=64)
-        g_codes = keep.tile([P, N], U32, name="g_codes", align_bytes=64)
-        g_scales = keep.tile([P, N], U8, name="g_scales", align_bytes=64)
-        for h, slots in enumerate(halves):
+        g_codes = keep.tile([P, HALF + N], U32, name="g_codes", align_bytes=64)
+        g_scales = keep.tile([P, HALF + N], U8, name="g_scales", align_bytes=64)
+        nc.gpsimd.memset(g_codes[:, 0:HALF], 0)
+        nc.gpsimd.memset(g_scales[:, 0:HALF], 0)
+
+        xm_scales = keep.tile([P, D], U8, name="xm_scales", align_bytes=64)
+        xm_codes = keep.tile([P, D], U32, name="xm_codes", align_bytes=64)
+        first_grouped = keep.tile([P, P, PACK], BF16, name="first_grouped", tag="x_then_xm", align_bytes=64)
+        group(nc.scalar.copy, first_grouped[:], xm_raw[:, :, 0:P])
+        rest_grouped = keep.tile([P, D - P, PACK], BF16, name="rest_grouped", align_bytes=64)
+
+        def form_g(h):
+            slots = halves[h]
+            g_grouped = keep.tile([P, HALF, PACK], BF16, name="g_grouped%d" % h, tag="g_grouped", align_bytes=64)
             nc.vector.tensor_tensor(
-                g_grouped[:, slots, :].rearrange("p (c i) s -> p c s i", i=2),
+                g_grouped[:].rearrange("p (c i) s -> p c s i", i=2),
                 scores[h][:].rearrange("p s (c i) -> p c s i", i=2),
                 target[:, :, slots].rearrange("p s (c i) -> p c s i", i=2),
                 SUBTRACT,
             )
-        for slots in halves:
-            quantize(g_codes[:, slots], g_scales[:, slots], g_grouped[:, slots, :], E5M2X4)
+            return g_grouped
 
-        xm_scales = keep.tile([P, D], U8, name="xm_scales", align_bytes=64)
+        def quantize_g(h, g_grouped):
+            cols = slice((h + 1) * HALF, (h + 2) * HALF)
+            quantize(g_codes[:, cols], g_scales[:, cols], g_grouped[:], E5M2X4)
 
-        def quantize_xm(e, grouped, codes):
-            feats = slice(e * P, (e + 1) * P)
-            group(nc.scalar.copy, grouped, xm_raw[:, :, feats])
-            quantize(codes, xm_scales[:, feats], grouped, E4M3X4)
-
-        def scatter_gradient(e, codes):
+        def gradient_pass(e, cols):
             feats = slice(e * P, (e + 1) * P)
             gradient_bank = psum.tile([P, N], F32, name="gradient_bank", tag="bank")
             nc.tensor.matmul_mx(
                 out=gradient_bank[:],
-                lhsT=codes.bitcast(E4M3X4),
+                lhsT=xm_codes[:, feats].bitcast(E4M3X4),
                 lhsT_scale=xm_scales[:, feats],
-                rhs=g_codes[:].bitcast(E5M2X4),
-                rhs_scale=g_scales[:],
+                rhs=g_codes[:, cols].bitcast(E5M2X4),
+                rhs_scale=g_scales[:, cols],
                 start=True,
                 stop=True,
             )
-            gradient = keep.tile([P, N], F32, name="gradient%d" % e)
-            nc.scalar.copy(gradient[:], gradient_bank[:])
-            window = windows[e % WINDOWS]
-            nc.vector.tensor_copy(window[:].indirect(offsets[:]), gradient[:])
-            nc.sync.dma_start(out[feats, :], window[:])
+            return gradient_bank
 
-        last = D // P - 1
-        xm_grouped = keep.tile([P, last * P, PACK], BF16, name="xm_grouped", tag="x_then_xm", align_bytes=64)
-        first_codes = keep.tile([P, P], U32, name="first_codes", tag="first_then_last", align_bytes=64)
-        later_codes = keep.tile([P, last * P], U32, name="later_codes", align_bytes=64)
-        xm_codes = [first_codes[:]] + [later_codes[:, k * P : (k + 1) * P] for k in range(last)]
-        for e in range(last):
-            quantize_xm(e, xm_grouped[:, e * P : (e + 1) * P, :], xm_codes[e])
-        scatter_gradient(0, xm_codes[0])
-        last_grouped = keep.tile([P, P, PACK], BF16, name="last_grouped", tag="first_then_last", align_bytes=64)
-        quantize_xm(last, last_grouped[:], xm_codes[last])
-        for e in range(1, last + 1):
-            scatter_gradient(e, xm_codes[e])
+        def scatter(e, bank_cols, slots, name):
+            gradient = keep.tile([P, slots.stop - slots.start], F32, name=name)
+            nc.scalar.copy(gradient[:], bank_cols)
+            listed = offsets[:, slots.start // BAND : slots.stop // BAND]
+            nc.vector.tensor_copy(windows[e % WINDOWS][:].indirect(listed), gradient[:])
+
+        g_first = form_g(0)
+        quantize_g(0, g_first)
+        quantize(xm_codes[:, 0:P], xm_scales[:, 0:P], first_grouped[:], E4M3X4)
+        padded_bank = gradient_pass(0, slice(0, N))
+        g_second = form_g(1)
+        quantize_g(1, g_second)
+        scatter(0, padded_bank[:, HALF:], halves[0], "gradient_first")
+        for e in range(1, D // P):
+            group(nc.scalar.copy, rest_grouped[:, (e - 1) * P : e * P, :], xm_raw[:, :, e * P : (e + 1) * P])
+        quantize(xm_codes[:, P : 2 * P], xm_scales[:, P : 2 * P], rest_grouped[:, 0:P, :], E4M3X4)
+        quantize(xm_codes[:, 2 * P :], xm_scales[:, 2 * P :], rest_grouped[:, P:, :], E4M3X4)
+        for e in range(D // P):
+            bank = gradient_pass(e, slice(HALF, HALF + N))
+            if e == 0:
+                scatter(e, bank[:, HALF:], halves[1], "gradient0")
+            else:
+                scatter(e, bank[:], slice(0, N), "gradient%d" % e)
+            nc.sync.dma_start(out[e * P : (e + 1) * P, :], windows[e % WINDOWS][:])

@@ -34,6 +34,7 @@ def tile_attend_gsq_w_kb_kernel(tc, xT, wT, y, wt, kb, xm, offs, out):
     with ExitStack() as ctx:
         keep = ctx.enter_context(tc.tile_pool(name="keep", bufs=1))
         shared = ctx.enter_context(tc.tile_pool(name="shared", bufs=1))
+        late = ctx.enter_context(tc.tile_pool(name="late", bufs=1))
         psum = ctx.enter_context(tc.psum_pool(name="psum", bufs=BANKS))
 
         def quantize(codes, scales, grouped, dtype):
@@ -55,10 +56,10 @@ def tile_attend_gsq_w_kb_kernel(tc, xT, wT, y, wt, kb, xm, offs, out):
         for t in range(1, PACK):
             nc.sync.dma_start(w_raw[t][:], w_planes[:, t, :])
 
-        x_planes = xT[0].rearrange("(p t) r -> p t r", t=PACK)
-        x_raw = [keep.tile([P, PACK, R // HALVES], F32, name="x_raw%d" % h) for h in range(HALVES)]
-        for h in range(HALVES):
-            nc.sync.dma_start(x_raw[h][:], x_planes[:, :, h * (R // HALVES) : (h + 1) * (R // HALVES)])
+        target_and_x = keep.tile([P, (PACK + 1) * N], F32, name="target_and_x", align_bytes=64)
+        target = target_and_x[:, 0 : PACK * N].rearrange("p (s n) -> p s n", s=PACK)
+        x_raw = target_and_x[:, N:].rearrange("p (t r) -> p t r", t=PACK)
+        nc.sync.dma_start(x_raw, xT[0].rearrange("(p t) r -> p t r", t=PACK))
 
         y_planes = y[0].rearrange("(p t) n -> p t n", t=PACK)
         y_pairs = [keep.tile([P, 2, N], F32, name="y_pair%d" % u) for u in range(2)]
@@ -66,8 +67,11 @@ def tile_attend_gsq_w_kb_kernel(tc, xT, wT, y, wt, kb, xm, offs, out):
             nc.sync.dma_start(y_pairs[u][:], y_planes[:, 2 * u : 2 * u + 2, :])
         y_raw = [y_pairs[t // 2][:, t % 2, :] for t in range(PACK)]
 
-        xm_raw = keep.tile([P, PACK, D], F32, name="xm_raw")
-        nc.sync.dma_start(xm_raw[:], xm[0].rearrange("(p t) d -> p t d", t=PACK))
+        xm_planes = xm[0].rearrange("(p t) d -> p t d", t=PACK)
+        xm_halves = [keep.tile([P, PACK, D // 2], F32, name="xm_half%d" % v) for v in range(2)]
+        for v in range(2):
+            nc.sync.dma_start(xm_halves[v][:], xm_planes[:, :, v * (D // 2) : (v + 1) * (D // 2)])
+        xm_raw = [xm_halves[e // 2][:, :, (e % 2) * P : (e % 2 + 1) * P] for e in range(D // P)]
 
         identity = keep.tile([P, P], F32, name="identity", tag="identity_then_window")
         make_identity(nc, identity[:])
@@ -112,44 +116,48 @@ def tile_attend_gsq_w_kb_kernel(tc, xT, wT, y, wt, kb, xm, offs, out):
         for slots in reversed(halves):
             listed = offsets[:, slots.start // BAND : slots.stop // BAND]
             nc.vector.tensor_copy(w_listed[1][:, 1, slots], w_raw[PACK - 1][:].indirect(listed))
-        w_codes = keep.tile([P, N], U32, name="w_codes", align_bytes=64)
+        w_codes = [
+            late.tile([P, HALF], U32, name="w_codes0", offset=0, align_bytes=64),
+            keep.tile([P, HALF], U32, name="w_codes1", align_bytes=64),
+        ]
         w_scales = keep.tile([P, N], U8, name="w_scales", align_bytes=64)
         group_pair(nc.scalar.copy, 1, 1)
         group_pair(nc.vector.tensor_copy, 1, 0)
         for h, slots in enumerate(halves):
-            quantize(w_codes[:, slots], w_scales[:, slots], w_grouped[h][:], E4M3X4)
+            quantize(w_codes[h][:], w_scales[:, slots], w_grouped[h][:], E4M3X4)
 
         x_grouped = [
             keep.tile([P, 2, P, PACK], BF16, name="x_grouped0", tag="kb_x_target", align_bytes=64),
             keep.tile([P, 2, P, PACK], BF16, name="x_grouped1", align_bytes=64),
         ]
-        m_half = P // HALVES
-        for h in range(HALVES):
-            for u in range(2):
-                copy = nc.vector.tensor_copy if (h, u) == (1, 0) else nc.scalar.copy
-                copy(
-                    x_grouped[u][:, :, h * m_half : (h + 1) * m_half, :].rearrange("p s m t -> p m t s"),
-                    x_raw[h][:].rearrange("p t (m s) -> p m t s", s=PACK)[:, :, :, 2 * u : 2 * u + 2],
-                )
-        x_codes = keep.tile([P, R], U32, name="x_codes", tag="x_then_xm", align_bytes=64)
+        for u, copy in enumerate((nc.vector.tensor_copy, nc.scalar.copy)):
+            copy(
+                x_grouped[u][:].rearrange("p s m t -> p m t s"),
+                x_raw.rearrange("p t (m s) -> p m t s", s=PACK)[:, :, :, 2 * u : 2 * u + 2],
+            )
+        x_codes = keep.tile([P, R], U32, name="x_codes", align_bytes=64)
         x_scales = keep.tile([P, R], U8, name="x_scales", align_bytes=64)
         for u in range(2):
             cols = slice(u * 2 * P, (u + 1) * 2 * P)
             quantize(x_codes[:, cols], x_scales[:, cols], x_grouped[u][:].rearrange("p s m t -> p (s m) t"), E4M3X4)
 
-        target = keep.tile([P, PACK, N], F32, name="target", tag="kb_x_target", align_bytes=64)
 
         def weigh_target(s, slots):
             nc.vector.scalar_tensor_tensor(
                 target[:, s, slots], y_raw[s][:, slots], row_weight[:, s : s + 1], kb_weighted[:, s, slots], MULT, SUBTRACT
             )
 
-        for s in range(PACK - 1):
+        for s in range(2):
             weigh_target(s, slice(0, N))
-        for slots in halves:
-            weigh_target(PACK - 1, slots)
+        weigh_target(2, halves[0])
+        weigh_target(3, halves[0])
+        weigh_target(2, halves[1])
 
-        scores = [keep.tile([P, PACK, HALF], F32, name="scores%d" % h) for h in range(HALVES)]
+        scores = [
+            keep.tile([P, PACK, HALF], F32, name="scores0"),
+            late.tile([P, PACK, HALF], F32, name="scores1", offset=0, align_bytes=64),
+        ]
+        first_grouped = keep.tile([P, P, PACK], BF16, name="first_grouped", align_bytes=64)
         for h, slots in enumerate(halves):
             for s in range(PACK):
                 rows = slice(s * P, (s + 1) * P)
@@ -158,11 +166,13 @@ def tile_attend_gsq_w_kb_kernel(tc, xT, wT, y, wt, kb, xm, offs, out):
                     out=score_bank[:],
                     lhsT=x_codes[:, rows].bitcast(E4M3X4),
                     lhsT_scale=x_scales[:, rows],
-                    rhs=w_codes[:, slots].bitcast(E4M3X4),
+                    rhs=w_codes[h][:].bitcast(E4M3X4),
                     rhs_scale=w_scales[:, slots],
                     start=True,
                     stop=True,
                 )
+                if (h, s) == (HALVES - 1, PACK - 1):
+                    group(nc.scalar.copy, first_grouped[:], xm_raw[0])
                 nc.scalar.activation(scores[h][:, s, :], score_bank[:], COPY, scale=row_weight[:, s : s + 1])
 
         g_codes = keep.tile([P, HALF + N], U32, name="g_codes", align_bytes=64)
@@ -172,9 +182,7 @@ def tile_attend_gsq_w_kb_kernel(tc, xT, wT, y, wt, kb, xm, offs, out):
 
         xm_scales = keep.tile([P, D], U8, name="xm_scales", align_bytes=64)
         xm_codes = keep.tile([P, D], U32, name="xm_codes", align_bytes=64)
-        first_grouped = keep.tile([P, P, PACK], BF16, name="first_grouped", tag="x_then_xm", align_bytes=64)
-        group(nc.scalar.copy, first_grouped[:], xm_raw[:, :, 0:P])
-        rest_grouped = keep.tile([P, D - P, PACK], BF16, name="rest_grouped", align_bytes=64)
+        second_grouped = keep.tile([P, P, PACK], BF16, name="second_grouped", align_bytes=64)
 
         def form_g(h):
             slots = halves[h]
@@ -205,27 +213,35 @@ def tile_attend_gsq_w_kb_kernel(tc, xT, wT, y, wt, kb, xm, offs, out):
             )
             return gradient_bank
 
-        def scatter(e, bank_cols, slots, name):
-            gradient = keep.tile([P, slots.stop - slots.start], F32, name=name)
+        def scatter(e, bank_cols, slots, gradient):
             nc.scalar.copy(gradient[:], bank_cols)
             listed = offsets[:, slots.start // BAND : slots.stop // BAND]
             nc.vector.tensor_copy(windows[e % WINDOWS][:].indirect(listed), gradient[:])
 
         g_first = form_g(0)
         quantize_g(0, g_first)
+        weigh_target(3, halves[1])
         quantize(xm_codes[:, 0:P], xm_scales[:, 0:P], first_grouped[:], E4M3X4)
-        padded_bank = gradient_pass(0, slice(0, N))
+        padded_banks = [gradient_pass(0, slice(0, N))]
         g_second = form_g(1)
         quantize_g(1, g_second)
-        scatter(0, padded_bank[:, HALF:], halves[0], "gradient_first")
-        for e in range(1, D // P):
-            group(nc.scalar.copy, rest_grouped[:, (e - 1) * P : e * P, :], xm_raw[:, :, e * P : (e + 1) * P])
-        quantize(xm_codes[:, P : 2 * P], xm_scales[:, P : 2 * P], rest_grouped[:, 0:P, :], E4M3X4)
-        quantize(xm_codes[:, 2 * P :], xm_scales[:, 2 * P :], rest_grouped[:, P:, :], E4M3X4)
+        group(nc.scalar.copy, second_grouped[:], xm_raw[1])
+        quantize(xm_codes[:, P : 2 * P], xm_scales[:, P : 2 * P], second_grouped[:], E4M3X4)
+        padded_banks.append(gradient_pass(1, slice(0, N)))
+        early_gradients = [
+            keep.tile([P, HALF], F32, name="early_gradient0"),
+            late.tile([P, HALF], F32, name="early_gradient1", offset=0),
+        ]
+        for e in range(2):
+            scatter(e, padded_banks[e][:, HALF:], halves[0], early_gradients[e])
         for e in range(D // P):
             bank = gradient_pass(e, slice(HALF, HALF + N))
-            if e == 0:
-                scatter(e, bank[:, HALF:], halves[1], "gradient0")
+            if e < 2:
+                scatter(e, bank[:, HALF:], halves[1], keep.tile([P, HALF], F32, name="gradient%d" % e))
             else:
-                scatter(e, bank[:], slice(0, N), "gradient%d" % e)
+                scatter(e, bank[:], slice(0, N), keep.tile([P, N], F32, name="gradient%d" % e))
             nc.sync.dma_start(out[e * P : (e + 1) * P, :], windows[e % WINDOWS][:])
+            if e == 0:
+                rest_grouped = late.tile([P, D // 2, PACK], BF16, name="rest_grouped", offset=1024, align_bytes=64)
+                group(nc.scalar.copy, rest_grouped[:], xm_halves[1][:])
+                quantize(xm_codes[:, 2 * P :], xm_scales[:, 2 * P :], rest_grouped[:], E4M3X4)

@@ -25,6 +25,9 @@ BANKS = 8
 HALVES = 2
 HALF = N // HALVES
 WINDOWS = 3
+G_SPLIT = 112
+G_WORDS = (N - G_SPLIT) * PACK // 2
+SCORES_AT = G_WORDS - 16
 
 
 def tile_attend_gsq_w_kb_kernel(tc, xT, wT, y, wt, kb, xm, offs, out):
@@ -56,9 +59,9 @@ def tile_attend_gsq_w_kb_kernel(tc, xT, wT, y, wt, kb, xm, offs, out):
         for t in range(1, PACK):
             nc.sync.dma_start(w_raw[t][:], w_planes[:, t, :])
 
-        target_and_x = keep.tile([P, (PACK + 1) * N], F32, name="target_and_x", align_bytes=64)
+        target_and_x = keep.tile([P, PACK * N + HALF], F32, name="target_and_x", align_bytes=64)
         target = target_and_x[:, 0 : PACK * N].rearrange("p (s n) -> p s n", s=PACK)
-        x_raw = target_and_x[:, N:].rearrange("p (t r) -> p t r", t=PACK)
+        x_raw = target_and_x[:, HALF:].rearrange("p (t r) -> p t r", t=PACK)
         nc.sync.dma_start(x_raw, xT[0].rearrange("(p t) r -> p t r", t=PACK))
 
         y_planes = y[0].rearrange("(p t) n -> p t n", t=PACK)
@@ -147,15 +150,14 @@ def tile_attend_gsq_w_kb_kernel(tc, xT, wT, y, wt, kb, xm, offs, out):
                 target[:, s, slots], y_raw[s][:, slots], row_weight[:, s : s + 1], kb_weighted[:, s, slots], MULT, SUBTRACT
             )
 
-        for s in range(2):
-            weigh_target(s, slice(0, N))
-        weigh_target(2, halves[0])
-        weigh_target(3, halves[0])
-        weigh_target(2, halves[1])
+        for s in range(PACK):
+            weigh_target(s, halves[0])
+        weigh_target(0, halves[1])
 
+        second_half = late.tile([P, SCORES_AT + PACK * HALF], F32, name="second_half", offset=0, align_bytes=64)
         scores = [
-            keep.tile([P, PACK, HALF], F32, name="scores0"),
-            late.tile([P, PACK, HALF], F32, name="scores1", offset=0, align_bytes=64),
+            keep.tile([P, PACK, HALF], F32, name="scores0")[:],
+            second_half[:, SCORES_AT : SCORES_AT + PACK * HALF].rearrange("p (s c) -> p s c", s=PACK),
         ]
         first_grouped = keep.tile([P, P, PACK], BF16, name="first_grouped", align_bytes=64)
         for h, slots in enumerate(halves):
@@ -171,7 +173,7 @@ def tile_attend_gsq_w_kb_kernel(tc, xT, wT, y, wt, kb, xm, offs, out):
                     start=True,
                     stop=True,
                 )
-                if (h, s) == (HALVES - 1, PACK - 1):
+                if (h, s) == (HALVES - 1, 0):
                     group(nc.scalar.copy, first_grouped[:], xm_raw[0])
                 nc.scalar.activation(scores[h][:, s, :], score_bank[:], COPY, scale=row_weight[:, s : s + 1])
 
@@ -182,22 +184,22 @@ def tile_attend_gsq_w_kb_kernel(tc, xT, wT, y, wt, kb, xm, offs, out):
 
         xm_scales = keep.tile([P, D], U8, name="xm_scales", align_bytes=64)
         xm_codes = keep.tile([P, D], U32, name="xm_codes", align_bytes=64)
-        second_grouped = keep.tile([P, P, PACK], BF16, name="second_grouped", align_bytes=64)
+        g_both = second_half[:, 0:G_WORDS].bitcast(BF16).rearrange("p (c s) -> p c s", s=PACK)
+        g_first = g_both[:, 0:HALF, :]
+        g_second = g_both[:, HALF - G_SPLIT :, :]
+        second_grouped = g_second[:, G_SPLIT : G_SPLIT + P, :]
 
-        def form_g(h):
-            slots = halves[h]
-            g_grouped = keep.tile([P, HALF, PACK], BF16, name="g_grouped%d" % h, tag="g_grouped", align_bytes=64)
-            nc.vector.tensor_tensor(
-                g_grouped[:].rearrange("p (c i) s -> p c s i", i=2),
-                scores[h][:].rearrange("p s (c i) -> p c s i", i=2),
-                target[:, :, slots].rearrange("p s (c i) -> p c s i", i=2),
+        def form_g(engine, h, g_grouped, part):
+            engine.tensor_tensor(
+                g_grouped[:, part, :].rearrange("p (c i) s -> p c s i", i=4),
+                scores[h][:, :, part].rearrange("p s (c i) -> p c s i", i=4),
+                target[:, :, halves[h]][:, :, part].rearrange("p s (c i) -> p c s i", i=4),
                 SUBTRACT,
             )
-            return g_grouped
 
         def quantize_g(h, g_grouped):
             cols = slice((h + 1) * HALF, (h + 2) * HALF)
-            quantize(g_codes[:, cols], g_scales[:, cols], g_grouped[:], E5M2X4)
+            quantize(g_codes[:, cols], g_scales[:, cols], g_grouped, E5M2X4)
 
         def gradient_pass(e, cols):
             feats = slice(e * P, (e + 1) * P)
@@ -214,34 +216,38 @@ def tile_attend_gsq_w_kb_kernel(tc, xT, wT, y, wt, kb, xm, offs, out):
             return gradient_bank
 
         def scatter(e, bank_cols, slots, gradient):
-            nc.scalar.copy(gradient[:], bank_cols)
+            nc.scalar.copy(gradient, bank_cols)
             listed = offsets[:, slots.start // BAND : slots.stop // BAND]
-            nc.vector.tensor_copy(windows[e % WINDOWS][:].indirect(listed), gradient[:])
+            nc.vector.tensor_copy(windows[e % WINDOWS][:].indirect(listed), gradient)
 
-        g_first = form_g(0)
+        form_g(nc.vector, 0, g_first, slice(0, HALF))
+        weigh_target(1, halves[1])
         quantize_g(0, g_first)
-        weigh_target(3, halves[1])
         quantize(xm_codes[:, 0:P], xm_scales[:, 0:P], first_grouped[:], E4M3X4)
         padded_banks = [gradient_pass(0, slice(0, N))]
-        g_second = form_g(1)
+        weigh_target(2, halves[1])
+        weigh_target(3, halves[1])
+        form_g(nc.vector, 1, g_second, slice(0, G_SPLIT))
+        group(nc.scalar.copy, second_grouped, xm_raw[1])
+        quantize(xm_codes[:, P : 2 * P], xm_scales[:, P : 2 * P], second_grouped, E4M3X4)
+        form_g(nc.gpsimd, 1, g_second, slice(G_SPLIT, HALF))
         quantize_g(1, g_second)
-        group(nc.scalar.copy, second_grouped[:], xm_raw[1])
-        quantize(xm_codes[:, P : 2 * P], xm_scales[:, P : 2 * P], second_grouped[:], E4M3X4)
         padded_banks.append(gradient_pass(1, slice(0, N)))
         early_gradients = [
-            keep.tile([P, HALF], F32, name="early_gradient0"),
-            late.tile([P, HALF], F32, name="early_gradient1", offset=0),
+            keep.tile([P, HALF], F32, name="early_gradient0")[:],
+            scores[1][:, 1, :],
         ]
         for e in range(2):
             scatter(e, padded_banks[e][:, HALF:], halves[0], early_gradients[e])
         for e in range(D // P):
             bank = gradient_pass(e, slice(HALF, HALF + N))
             if e < 2:
-                scatter(e, bank[:, HALF:], halves[1], keep.tile([P, HALF], F32, name="gradient%d" % e))
+                scatter(e, bank[:, HALF:], halves[1], keep.tile([P, HALF], F32, name="gradient%d" % e)[:])
             else:
-                scatter(e, bank[:], slice(0, N), keep.tile([P, N], F32, name="gradient%d" % e))
+                scatter(e, bank[:], slice(0, N), keep.tile([P, N], F32, name="gradient%d" % e)[:])
             nc.sync.dma_start(out[e * P : (e + 1) * P, :], windows[e % WINDOWS][:])
             if e == 0:
-                rest_grouped = late.tile([P, D // 2, PACK], BF16, name="rest_grouped", offset=1024, align_bytes=64)
-                group(nc.scalar.copy, rest_grouped[:], xm_halves[1][:])
-                quantize(xm_codes[:, 2 * P :], xm_scales[:, 2 * P :], rest_grouped[:], E4M3X4)
+                rest_words = second_half[:, SCORES_AT + 2 * HALF :]
+                rest_grouped = rest_words.bitcast(BF16).rearrange("p (c t) -> p c t", t=PACK)
+                group(nc.scalar.copy, rest_grouped, xm_halves[1][:])
+                quantize(xm_codes[:, 2 * P :], xm_scales[:, 2 * P :], rest_grouped, E4M3X4)

@@ -16,6 +16,7 @@ E4M3X4 = mybir.dt.float8_e4m3fn_x4
 E5M2X4 = mybir.dt.float8_e5m2_x4
 COPY = mybir.ActivationFunctionType.Copy
 MULT = mybir.AluOpType.mult
+ADD = mybir.AluOpType.add
 SUBTRACT = mybir.AluOpType.subtract
 
 P = 128
@@ -25,9 +26,8 @@ BANKS = 8
 HALVES = 2
 HALF = N // HALVES
 WINDOWS = 3
-G_SPLIT = 112
-G_WORDS = (N - G_SPLIT) * PACK // 2
-SCORES_AT = G_WORDS - 16
+G_SPLIT = 128
+X_SPLIT = 96
 
 
 def tile_attend_gsq_w_kb_kernel(tc, xT, wT, y, wt, kb, xm, offs, out):
@@ -37,7 +37,6 @@ def tile_attend_gsq_w_kb_kernel(tc, xT, wT, y, wt, kb, xm, offs, out):
     with ExitStack() as ctx:
         keep = ctx.enter_context(tc.tile_pool(name="keep", bufs=1))
         shared = ctx.enter_context(tc.tile_pool(name="shared", bufs=1))
-        late = ctx.enter_context(tc.tile_pool(name="late", bufs=1))
         psum = ctx.enter_context(tc.psum_pool(name="psum", bufs=BANKS))
 
         def quantize(codes, scales, grouped, dtype):
@@ -59,9 +58,14 @@ def tile_attend_gsq_w_kb_kernel(tc, xT, wT, y, wt, kb, xm, offs, out):
         for t in range(1, PACK):
             nc.sync.dma_start(w_raw[t][:], w_planes[:, t, :])
 
-        target_and_x = keep.tile([P, PACK * N + HALF], F32, name="target_and_x", align_bytes=64)
-        target = target_and_x[:, 0 : PACK * N].rearrange("p (s n) -> p s n", s=PACK)
-        x_raw = target_and_x[:, HALF:].rearrange("p (t r) -> p t r", t=PACK)
+        work = keep.tile([P, 12 * HALF], F32, name="work", align_bytes=64)
+
+        def planes_at(first):
+            return work[:, first * HALF : (first + PACK) * HALF].rearrange("p (s c) -> p s c", s=PACK)
+
+        target = [planes_at(0), planes_at(4)]
+        scores = [planes_at(6), planes_at(8)]
+        x_raw = work[:, 0 : PACK * R].rearrange("p (t r) -> p t r", t=PACK)
         nc.sync.dma_start(x_raw, xT[0].rearrange("(p t) r -> p t r", t=PACK))
 
         y_planes = y[0].rearrange("(p t) n -> p t n", t=PACK)
@@ -119,13 +123,11 @@ def tile_attend_gsq_w_kb_kernel(tc, xT, wT, y, wt, kb, xm, offs, out):
         for slots in reversed(halves):
             listed = offsets[:, slots.start // BAND : slots.stop // BAND]
             nc.vector.tensor_copy(w_listed[1][:, 1, slots], w_raw[PACK - 1][:].indirect(listed))
-        w_codes = [
-            late.tile([P, HALF], U32, name="w_codes0", offset=0, align_bytes=64),
-            keep.tile([P, HALF], U32, name="w_codes1", align_bytes=64),
-        ]
+        w_codes = [keep.tile([P, HALF], U32, name="w_codes0", align_bytes=64)]
         w_scales = keep.tile([P, N], U8, name="w_scales", align_bytes=64)
         group_pair(nc.scalar.copy, 1, 1)
         group_pair(nc.vector.tensor_copy, 1, 0)
+        w_codes.append(keep.tile([P, HALF], U32, name="w_codes1", align_bytes=64))
         for h, slots in enumerate(halves):
             quantize(w_codes[h][:], w_scales[:, slots], w_grouped[h][:], E4M3X4)
 
@@ -133,11 +135,16 @@ def tile_attend_gsq_w_kb_kernel(tc, xT, wT, y, wt, kb, xm, offs, out):
             keep.tile([P, 2, P, PACK], BF16, name="x_grouped0", tag="kb_x_target", align_bytes=64),
             keep.tile([P, 2, P, PACK], BF16, name="x_grouped1", align_bytes=64),
         ]
-        for u, copy in enumerate((nc.vector.tensor_copy, nc.scalar.copy)):
+
+        def deal_x(copy, u, m):
             copy(
-                x_grouped[u][:].rearrange("p s m t -> p m t s"),
-                x_raw.rearrange("p t (m s) -> p m t s", s=PACK)[:, :, :, 2 * u : 2 * u + 2],
+                x_grouped[u][:].rearrange("p s m t -> p m t s")[:, m],
+                x_raw.rearrange("p t (m s) -> p m t s", s=PACK)[:, m, :, 2 * u : 2 * u + 2],
             )
+
+        deal_x(nc.vector.tensor_copy, 0, slice(0, P))
+        deal_x(nc.scalar.copy, 1, slice(0, X_SPLIT))
+        deal_x(nc.vector.tensor_copy, 1, slice(X_SPLIT, P))
         x_codes = keep.tile([P, R], U32, name="x_codes", align_bytes=64)
         x_scales = keep.tile([P, R], U8, name="x_scales", align_bytes=64)
         for u in range(2):
@@ -145,25 +152,39 @@ def tile_attend_gsq_w_kb_kernel(tc, xT, wT, y, wt, kb, xm, offs, out):
             quantize(x_codes[:, cols], x_scales[:, cols], x_grouped[u][:].rearrange("p s m t -> p (s m) t"), E4M3X4)
 
 
-        def weigh_target(s, slots):
+        def weigh_target(s, h, part):
             nc.vector.scalar_tensor_tensor(
-                target[:, s, slots], y_raw[s][:, slots], row_weight[:, s : s + 1], kb_weighted[:, s, slots], MULT, SUBTRACT
+                target[h][:, s, part],
+                y_raw[s][:, halves[h]][:, part],
+                row_weight[:, s : s + 1],
+                kb_weighted[:, s, halves[h]][:, part],
+                MULT,
+                SUBTRACT,
             )
 
-        for s in range(PACK):
-            weigh_target(s, halves[0])
-        weigh_target(0, halves[1])
+        for s in range(2):
+            both = work[:, 0 : 8 * HALF].rearrange("p (h s c) -> p s h c", h=HALVES, s=PACK)[:, s]
+            nc.scalar.activation(
+                both, y_raw[s].rearrange("p (h c) -> p h c", h=HALVES), COPY, scale=row_weight[:, s : s + 1]
+            )
 
-        second_half = late.tile([P, SCORES_AT + PACK * HALF], F32, name="second_half", offset=0, align_bytes=64)
-        scores = [
-            keep.tile([P, PACK, HALF], F32, name="scores0")[:],
-            second_half[:, SCORES_AT : SCORES_AT + PACK * HALF].rearrange("p (s c) -> p s c", s=PACK),
-        ]
         first_grouped = keep.tile([P, P, PACK], BF16, name="first_grouped", align_bytes=64)
+        score_banks = {}
+
+        def empty_scores(h, s):
+            weight = row_weight[:, s : s + 1]
+            if s < 2:
+                nc.vector.scalar_tensor_tensor(
+                    scores[h][:, s, :], score_banks[h, s][:], weight, kb_weighted[:, s, halves[h]], MULT, ADD
+                )
+            else:
+                nc.scalar.activation(scores[h][:, s, :], score_banks[h, s][:], COPY, scale=weight)
+
         for h, slots in enumerate(halves):
             for s in range(PACK):
                 rows = slice(s * P, (s + 1) * P)
                 score_bank = psum.tile([P, HALF], F32, name="score_bank", tag="bank")
+                score_banks[h, s] = score_bank
                 nc.tensor.matmul_mx(
                     out=score_bank[:],
                     lhsT=x_codes[:, rows].bitcast(E4M3X4),
@@ -173,9 +194,14 @@ def tile_attend_gsq_w_kb_kernel(tc, xT, wT, y, wt, kb, xm, offs, out):
                     start=True,
                     stop=True,
                 )
-                if (h, s) == (HALVES - 1, 0):
-                    group(nc.scalar.copy, first_grouped[:], xm_raw[0])
-                nc.scalar.activation(scores[h][:, s, :], score_bank[:], COPY, scale=row_weight[:, s : s + 1])
+        for s in range(PACK):
+            empty_scores(0, s)
+        weigh_target(2, 0, slice(0, HALF))
+        weigh_target(3, 0, slice(0, P))
+        weigh_target(3, 0, slice(P, HALF))
+        group(nc.scalar.copy, first_grouped[:], xm_raw[0])
+        for s in range(2, PACK):
+            empty_scores(1, s)
 
         g_codes = keep.tile([P, HALF + N], U32, name="g_codes", align_bytes=64)
         g_scales = keep.tile([P, HALF + N], U8, name="g_scales", align_bytes=64)
@@ -184,16 +210,16 @@ def tile_attend_gsq_w_kb_kernel(tc, xT, wT, y, wt, kb, xm, offs, out):
 
         xm_scales = keep.tile([P, D], U8, name="xm_scales", align_bytes=64)
         xm_codes = keep.tile([P, D], U32, name="xm_codes", align_bytes=64)
-        g_both = second_half[:, 0:G_WORDS].bitcast(BF16).rearrange("p (c s) -> p c s", s=PACK)
-        g_first = g_both[:, 0:HALF, :]
-        g_second = g_both[:, HALF - G_SPLIT :, :]
-        second_grouped = g_second[:, G_SPLIT : G_SPLIT + P, :]
+        g_first = keep.tile([P, HALF, PACK], BF16, name="g_first", align_bytes=64)[:]
+        g_words = work[:, 2 * HALF + 16 : 4 * HALF + 16]
+        g_second = g_words.bitcast(BF16).rearrange("p (c s) -> p c s", s=PACK)
+        second_grouped = g_second[:, HALF - 8 - P : HALF - 8, :]
 
         def form_g(engine, h, g_grouped, part):
             engine.tensor_tensor(
                 g_grouped[:, part, :].rearrange("p (c i) s -> p c s i", i=4),
                 scores[h][:, :, part].rearrange("p s (c i) -> p c s i", i=4),
-                target[:, :, halves[h]][:, :, part].rearrange("p s (c i) -> p c s i", i=4),
+                target[h][:, :, part].rearrange("p s (c i) -> p c s i", i=4),
                 SUBTRACT,
             )
 
@@ -220,21 +246,22 @@ def tile_attend_gsq_w_kb_kernel(tc, xT, wT, y, wt, kb, xm, offs, out):
             listed = offsets[:, slots.start // BAND : slots.stop // BAND]
             nc.vector.tensor_copy(windows[e % WINDOWS][:].indirect(listed), gradient)
 
-        form_g(nc.vector, 0, g_first, slice(0, HALF))
-        weigh_target(1, halves[1])
-        quantize_g(0, g_first)
+        form_g(nc.vector, 0, g_first, slice(0, P))
+        form_g(nc.vector, 0, g_first, slice(P, HALF))
         quantize(xm_codes[:, 0:P], xm_scales[:, 0:P], first_grouped[:], E4M3X4)
+        quantize_g(0, g_first)
         padded_banks = [gradient_pass(0, slice(0, N))]
-        weigh_target(2, halves[1])
-        weigh_target(3, halves[1])
-        form_g(nc.vector, 1, g_second, slice(0, G_SPLIT))
+        for s in range(2):
+            weigh_target(s + 2, 1, slice(0, HALF))
+            empty_scores(1, s)
         group(nc.scalar.copy, second_grouped, xm_raw[1])
         quantize(xm_codes[:, P : 2 * P], xm_scales[:, P : 2 * P], second_grouped, E4M3X4)
+        form_g(nc.vector, 1, g_second, slice(0, G_SPLIT))
         form_g(nc.gpsimd, 1, g_second, slice(G_SPLIT, HALF))
         quantize_g(1, g_second)
         padded_banks.append(gradient_pass(1, slice(0, N)))
         early_gradients = [
-            keep.tile([P, HALF], F32, name="early_gradient0")[:],
+            y_raw[3][:, halves[1]],
             scores[1][:, 1, :],
         ]
         for e in range(2):
@@ -247,7 +274,7 @@ def tile_attend_gsq_w_kb_kernel(tc, xT, wT, y, wt, kb, xm, offs, out):
                 scatter(e, bank[:], slice(0, N), keep.tile([P, N], F32, name="gradient%d" % e)[:])
             nc.sync.dma_start(out[e * P : (e + 1) * P, :], windows[e % WINDOWS][:])
             if e == 0:
-                rest_words = second_half[:, SCORES_AT + 2 * HALF :]
+                rest_words = work[:, 10 * HALF :]
                 rest_grouped = rest_words.bitcast(BF16).rearrange("p (c t) -> p c t", t=PACK)
                 group(nc.scalar.copy, rest_grouped, xm_halves[1][:])
                 quantize(xm_codes[:, 2 * P :], xm_scales[:, 2 * P :], rest_grouped, E4M3X4)

@@ -26,8 +26,7 @@ BANKS = 8
 HALVES = 2
 HALF = N // HALVES
 WINDOWS = 3
-G_SPLIT = 128
-X_SPLIT = 96
+G_SPLIT = 120
 
 
 def tile_attend_gsq_w_kb_kernel(tc, xT, wT, y, wt, kb, xm, offs, out):
@@ -58,13 +57,13 @@ def tile_attend_gsq_w_kb_kernel(tc, xT, wT, y, wt, kb, xm, offs, out):
         for t in range(1, PACK):
             nc.sync.dma_start(w_raw[t][:], w_planes[:, t, :])
 
-        work = keep.tile([P, 12 * HALF], F32, name="work", align_bytes=64)
+        work = keep.tile([P, 20 * HALF], F32, name="work", align_bytes=64)
 
         def planes_at(first):
             return work[:, first * HALF : (first + PACK) * HALF].rearrange("p (s c) -> p s c", s=PACK)
 
-        target = [planes_at(0), planes_at(4)]
-        scores = [planes_at(6), planes_at(8)]
+        target = [planes_at(6), planes_at(10)]
+        scores = [planes_at(12), planes_at(14)]
         x_raw = work[:, 0 : PACK * R].rearrange("p (t r) -> p t r", t=PACK)
         nc.sync.dma_start(x_raw, xT[0].rearrange("(p t) r -> p t r", t=PACK))
 
@@ -100,9 +99,13 @@ def tile_attend_gsq_w_kb_kernel(tc, xT, wT, y, wt, kb, xm, offs, out):
 
         kb_listed = keep.tile([P, N], F32, name="kb_listed", tag="kb_x_target", align_bytes=64)
         nc.vector.tensor_copy(kb_listed[:], kb_window[:].indirect(offsets[:]))
-        kb_weighted = keep.tile([P, PACK, N], F32, name="kb_weighted")
+        kb_late = keep.tile([P, 2, HALVES, HALF], F32, name="kb_late")
+        kb_early = work[:, 8 * HALF :].rearrange("p (u c) -> p u c", c=HALF)
+        kb_weighted = [kb_early[:, 0::10, :], kb_early[:, 1::10, :], kb_late[:, 0], kb_late[:, 1]]
         for t in range(PACK):
-            nc.scalar.activation(kb_weighted[:, t, :], kb_listed[:], COPY, scale=row_weight[:, t : t + 1])
+            nc.scalar.activation(
+                kb_weighted[t], kb_listed[:].rearrange("p (h c) -> p h c", h=HALVES), COPY, scale=row_weight[:, t : t + 1]
+            )
 
         w_listed = [
             shared.tile([P, 2, N], BF16, name="w_listed0", offset=6144, align_bytes=64),
@@ -123,7 +126,7 @@ def tile_attend_gsq_w_kb_kernel(tc, xT, wT, y, wt, kb, xm, offs, out):
         for slots in reversed(halves):
             listed = offsets[:, slots.start // BAND : slots.stop // BAND]
             nc.vector.tensor_copy(w_listed[1][:, 1, slots], w_raw[PACK - 1][:].indirect(listed))
-        w_codes = [keep.tile([P, HALF], U32, name="w_codes0", align_bytes=64)]
+        w_codes = [keep.tile([P, HALF], U32, name="w_codes0", tag="w_then_xm", align_bytes=64)]
         w_scales = keep.tile([P, N], U8, name="w_scales", align_bytes=64)
         group_pair(nc.scalar.copy, 1, 1)
         group_pair(nc.vector.tensor_copy, 1, 0)
@@ -132,24 +135,23 @@ def tile_attend_gsq_w_kb_kernel(tc, xT, wT, y, wt, kb, xm, offs, out):
             quantize(w_codes[h][:], w_scales[:, slots], w_grouped[h][:], E4M3X4)
 
         x_grouped = [
-            keep.tile([P, 2, P, PACK], BF16, name="x_grouped0", tag="kb_x_target", align_bytes=64),
-            keep.tile([P, 2, P, PACK], BF16, name="x_grouped1", align_bytes=64),
+            keep.tile([P, 2, P, PACK], BF16, name="x_grouped0", tag="kb_x_target", align_bytes=64)[:],
+            work[:, 12 * HALF : 14 * HALF].bitcast(BF16).rearrange("p (s m t) -> p s m t", s=2, t=PACK),
         ]
 
         def deal_x(copy, u, m):
             copy(
-                x_grouped[u][:].rearrange("p s m t -> p m t s")[:, m],
+                x_grouped[u].rearrange("p s m t -> p m t s")[:, m],
                 x_raw.rearrange("p t (m s) -> p m t s", s=PACK)[:, m, :, 2 * u : 2 * u + 2],
             )
 
         deal_x(nc.vector.tensor_copy, 0, slice(0, P))
-        deal_x(nc.scalar.copy, 1, slice(0, X_SPLIT))
-        deal_x(nc.vector.tensor_copy, 1, slice(X_SPLIT, P))
+        deal_x(nc.scalar.copy, 1, slice(0, P))
         x_codes = keep.tile([P, R], U32, name="x_codes", align_bytes=64)
         x_scales = keep.tile([P, R], U8, name="x_scales", align_bytes=64)
         for u in range(2):
             cols = slice(u * 2 * P, (u + 1) * 2 * P)
-            quantize(x_codes[:, cols], x_scales[:, cols], x_grouped[u][:].rearrange("p s m t -> p (s m) t"), E4M3X4)
+            quantize(x_codes[:, cols], x_scales[:, cols], x_grouped[u].rearrange("p s m t -> p (s m) t"), E4M3X4)
 
 
         def weigh_target(s, h, part):
@@ -157,25 +159,25 @@ def tile_attend_gsq_w_kb_kernel(tc, xT, wT, y, wt, kb, xm, offs, out):
                 target[h][:, s, part],
                 y_raw[s][:, halves[h]][:, part],
                 row_weight[:, s : s + 1],
-                kb_weighted[:, s, halves[h]][:, part],
+                kb_weighted[s][:, h, part],
                 MULT,
                 SUBTRACT,
             )
 
         for s in range(2):
-            both = work[:, 0 : 8 * HALF].rearrange("p (h s c) -> p s h c", h=HALVES, s=PACK)[:, s]
+            both = work[:, 6 * HALF : 14 * HALF].rearrange("p (h s c) -> p s h c", h=HALVES, s=PACK)[:, s]
             nc.scalar.activation(
                 both, y_raw[s].rearrange("p (h c) -> p h c", h=HALVES), COPY, scale=row_weight[:, s : s + 1]
             )
 
-        first_grouped = keep.tile([P, P, PACK], BF16, name="first_grouped", align_bytes=64)
+        first_grouped = keep.tile([P, P, PACK], BF16, name="first_grouped", tag="w_then_xm", align_bytes=64)
         score_banks = {}
 
         def empty_scores(h, s):
             weight = row_weight[:, s : s + 1]
             if s < 2:
                 nc.vector.scalar_tensor_tensor(
-                    scores[h][:, s, :], score_banks[h, s][:], weight, kb_weighted[:, s, halves[h]], MULT, ADD
+                    scores[h][:, s, :], score_banks[h, s][:], weight, kb_weighted[s][:, h, :], MULT, ADD
                 )
             else:
                 nc.scalar.activation(scores[h][:, s, :], score_banks[h, s][:], COPY, scale=weight)
@@ -211,7 +213,7 @@ def tile_attend_gsq_w_kb_kernel(tc, xT, wT, y, wt, kb, xm, offs, out):
         xm_scales = keep.tile([P, D], U8, name="xm_scales", align_bytes=64)
         xm_codes = keep.tile([P, D], U32, name="xm_codes", align_bytes=64)
         g_first = keep.tile([P, HALF, PACK], BF16, name="g_first", align_bytes=64)[:]
-        g_words = work[:, 2 * HALF + 16 : 4 * HALF + 16]
+        g_words = work[:, 8 * HALF + 16 : 10 * HALF + 16]
         g_second = g_words.bitcast(BF16).rearrange("p (c s) -> p c s", s=PACK)
         second_grouped = g_second[:, HALF - 8 - P : HALF - 8, :]
 
@@ -274,7 +276,7 @@ def tile_attend_gsq_w_kb_kernel(tc, xT, wT, y, wt, kb, xm, offs, out):
                 scatter(e, bank[:], slice(0, N), keep.tile([P, N], F32, name="gradient%d" % e)[:])
             nc.sync.dma_start(out[e * P : (e + 1) * P, :], windows[e % WINDOWS][:])
             if e == 0:
-                rest_words = work[:, 10 * HALF :]
+                rest_words = work[:, 16 * HALF : 18 * HALF]
                 rest_grouped = rest_words.bitcast(BF16).rearrange("p (c t) -> p c t", t=PACK)
                 group(nc.scalar.copy, rest_grouped, xm_halves[1][:])
                 quantize(xm_codes[:, 2 * P :], xm_scales[:, 2 * P :], rest_grouped, E4M3X4)

@@ -26,7 +26,8 @@ BANKS = 8
 HALVES = 2
 HALF = N // HALVES
 WINDOWS = 3
-G_SPLIT = 120
+G_SPLIT = 160
+SCORE_BANKS = ((4, 5, 6, 7), (6, 0, 1, 2))
 
 
 def tile_attend_gsq_w_kb_kernel(tc, xT, wT, y, wt, kb, xm, offs, out):
@@ -36,7 +37,7 @@ def tile_attend_gsq_w_kb_kernel(tc, xT, wT, y, wt, kb, xm, offs, out):
     with ExitStack() as ctx:
         keep = ctx.enter_context(tc.tile_pool(name="keep", bufs=1))
         shared = ctx.enter_context(tc.tile_pool(name="shared", bufs=1))
-        psum = ctx.enter_context(tc.psum_pool(name="psum", bufs=BANKS))
+        psum = ctx.enter_context(tc.psum_pool(name="psum", bufs=1))
 
         def quantize(codes, scales, grouped, dtype):
             nc.vector.quantize_mx(out=codes.bitcast(dtype), scales=scales, in_=grouped.rearrange("p c t -> p (c t)"))
@@ -57,14 +58,14 @@ def tile_attend_gsq_w_kb_kernel(tc, xT, wT, y, wt, kb, xm, offs, out):
         for t in range(1, PACK):
             nc.sync.dma_start(w_raw[t][:], w_planes[:, t, :])
 
-        work = keep.tile([P, 20 * HALF], F32, name="work", align_bytes=64)
+        work = keep.tile([P, 19 * HALF], F32, name="work", align_bytes=64)
 
         def planes_at(first):
             return work[:, first * HALF : (first + PACK) * HALF].rearrange("p (s c) -> p s c", s=PACK)
 
-        target = [planes_at(6), planes_at(10)]
-        scores = [planes_at(12), planes_at(14)]
-        x_raw = work[:, 0 : PACK * R].rearrange("p (t r) -> p t r", t=PACK)
+        target = [planes_at(0), planes_at(4)]
+        scores = [work[:, 7 * HALF :].rearrange("p (s u c) -> p s u c", s=PACK, c=HALF)[:, :, 0, :], planes_at(9)]
+        x_raw = work[:, HALF : HALF + PACK * R].rearrange("p (t r) -> p t r", t=PACK)
         nc.sync.dma_start(x_raw, xT[0].rearrange("(p t) r -> p t r", t=PACK))
 
         y_planes = y[0].rearrange("(p t) n -> p t n", t=PACK)
@@ -88,7 +89,7 @@ def tile_attend_gsq_w_kb_kernel(tc, xT, wT, y, wt, kb, xm, offs, out):
         kb_items = kb_window[:].rearrange("p (n c) -> p n c", n=P)
         turns_per_bank = N // P
         for c0 in range(0, T // P, turns_per_bank):
-            spread = psum.tile([P, turns_per_bank, P], F32, name="spread", tag="bank")
+            spread = psum.tile([P, turns_per_bank, P], F32, name="spread", tag="bank%d" % (c0 // turns_per_bank))
             for c in range(turns_per_bank):
                 column = kb_columns[:, c0 + c : c0 + c + 1]
                 nc.tensor.transpose(spread[:, c, :], column.to_broadcast([P, P]), identity[:])
@@ -99,12 +100,10 @@ def tile_attend_gsq_w_kb_kernel(tc, xT, wT, y, wt, kb, xm, offs, out):
 
         kb_listed = keep.tile([P, N], F32, name="kb_listed", tag="kb_x_target", align_bytes=64)
         nc.vector.tensor_copy(kb_listed[:], kb_window[:].indirect(offsets[:]))
-        kb_late = keep.tile([P, 2, HALVES, HALF], F32, name="kb_late")
-        kb_early = work[:, 8 * HALF :].rearrange("p (u c) -> p u c", c=HALF)
-        kb_weighted = [kb_early[:, 0::10, :], kb_early[:, 1::10, :], kb_late[:, 0], kb_late[:, 1]]
+        kb_weighted = keep.tile([P, PACK, HALVES, HALF], F32, name="kb_weighted")
         for t in range(PACK):
             nc.scalar.activation(
-                kb_weighted[t], kb_listed[:].rearrange("p (h c) -> p h c", h=HALVES), COPY, scale=row_weight[:, t : t + 1]
+                kb_weighted[:, t].rearrange("p h c -> p (h c)"), kb_listed[:], COPY, scale=row_weight[:, t : t + 1]
             )
 
         w_listed = [
@@ -123,20 +122,20 @@ def tile_attend_gsq_w_kb_kernel(tc, xT, wT, y, wt, kb, xm, offs, out):
             nc.vector.tensor_copy(w_listed[t // 2][:, t % 2, :], w_raw[t][:].indirect(offsets[:]))
         for h in range(HALVES):
             group_pair(nc.scalar.copy, 0, h)
-        for slots in reversed(halves):
+        for slots in halves:
             listed = offsets[:, slots.start // BAND : slots.stop // BAND]
             nc.vector.tensor_copy(w_listed[1][:, 1, slots], w_raw[PACK - 1][:].indirect(listed))
-        w_codes = [keep.tile([P, HALF], U32, name="w_codes0", tag="w_then_xm", align_bytes=64)]
+        w_codes = [keep.tile([P, HALF], U32, name="w_codes0", tag="w_then_xm", align_bytes=64)[:]]
         w_scales = keep.tile([P, N], U8, name="w_scales", align_bytes=64)
         group_pair(nc.scalar.copy, 1, 1)
         group_pair(nc.vector.tensor_copy, 1, 0)
-        w_codes.append(keep.tile([P, HALF], U32, name="w_codes1", align_bytes=64))
+        w_codes.append(keep.tile([P, HALF], U32, name="w_codes1", align_bytes=64)[:])
         for h, slots in enumerate(halves):
-            quantize(w_codes[h][:], w_scales[:, slots], w_grouped[h][:], E4M3X4)
+            quantize(w_codes[h], w_scales[:, slots], w_grouped[h][:], E4M3X4)
 
         x_grouped = [
             keep.tile([P, 2, P, PACK], BF16, name="x_grouped0", tag="kb_x_target", align_bytes=64)[:],
-            work[:, 12 * HALF : 14 * HALF].bitcast(BF16).rearrange("p (s m t) -> p s m t", s=2, t=PACK),
+            work[:, 10 * HALF : 12 * HALF].bitcast(BF16).rearrange("p (s m t) -> p s m t", s=2, t=PACK),
         ]
 
         def deal_x(copy, u, m):
@@ -154,56 +153,65 @@ def tile_attend_gsq_w_kb_kernel(tc, xT, wT, y, wt, kb, xm, offs, out):
             quantize(x_codes[:, cols], x_scales[:, cols], x_grouped[u].rearrange("p s m t -> p (s m) t"), E4M3X4)
 
 
-        def weigh_target(s, h, part):
+        targets = work[:, 0 : 8 * HALF].rearrange("p (h s c) -> p s h c", h=HALVES, s=PACK)
+        first, second, both = slice(0, 1), slice(1, 2), slice(0, 2)
+
+        def y_part(s, hs):
+            return y_raw[s].rearrange("p (h c) -> p h c", h=HALVES)[:, hs]
+
+        def weigh_target(s, hs):
             nc.vector.scalar_tensor_tensor(
-                target[h][:, s, part],
-                y_raw[s][:, halves[h]][:, part],
-                row_weight[:, s : s + 1],
-                kb_weighted[s][:, h, part],
-                MULT,
-                SUBTRACT,
+                targets[:, s, hs], y_part(s, hs), row_weight[:, s : s + 1], kb_weighted[:, s, hs], MULT, SUBTRACT
             )
 
-        for s in range(2):
-            both = work[:, 6 * HALF : 14 * HALF].rearrange("p (h s c) -> p s h c", h=HALVES, s=PACK)[:, s]
-            nc.scalar.activation(
-                both, y_raw[s].rearrange("p (h c) -> p h c", h=HALVES), COPY, scale=row_weight[:, s : s + 1]
-            )
+        def weigh_y(s, hs):
+            nc.scalar.activation(targets[:, s, hs], y_part(s, hs), COPY, scale=row_weight[:, s : s + 1])
+
+        weigh_target(0, first)
+        weigh_target(0, second)
+        weigh_y(1, both)
 
         first_grouped = keep.tile([P, P, PACK], BF16, name="first_grouped", tag="w_then_xm", align_bytes=64)
         score_banks = {}
 
-        def empty_scores(h, s):
-            weight = row_weight[:, s : s + 1]
-            if s < 2:
-                nc.vector.scalar_tensor_tensor(
-                    scores[h][:, s, :], score_banks[h, s][:], weight, kb_weighted[s][:, h, :], MULT, ADD
-                )
-            else:
-                nc.scalar.activation(scores[h][:, s, :], score_banks[h, s][:], COPY, scale=weight)
+        def weigh_scores(h, s):
+            nc.scalar.activation(scores[h][:, s, :], score_banks[h, s][:], COPY, scale=row_weight[:, s : s + 1])
+
+        def bias_scores(h, s, part):
+            nc.vector.scalar_tensor_tensor(
+                scores[h][:, s, part],
+                score_banks[h, s][:, part],
+                row_weight[:, s : s + 1],
+                kb_weighted[:, s, h, part],
+                MULT,
+                ADD,
+            )
 
         for h, slots in enumerate(halves):
             for s in range(PACK):
                 rows = slice(s * P, (s + 1) * P)
-                score_bank = psum.tile([P, HALF], F32, name="score_bank", tag="bank")
+                score_bank = psum.tile([P, HALF], F32, name="score_bank", tag="bank%d" % SCORE_BANKS[h][s])
                 score_banks[h, s] = score_bank
                 nc.tensor.matmul_mx(
                     out=score_bank[:],
                     lhsT=x_codes[:, rows].bitcast(E4M3X4),
                     lhsT_scale=x_scales[:, rows],
-                    rhs=w_codes[h][:].bitcast(E4M3X4),
+                    rhs=w_codes[h].bitcast(E4M3X4),
                     rhs_scale=w_scales[:, slots],
                     start=True,
                     stop=True,
                 )
-        for s in range(PACK):
-            empty_scores(0, s)
-        weigh_target(2, 0, slice(0, HALF))
-        weigh_target(3, 0, slice(0, P))
-        weigh_target(3, 0, slice(P, HALF))
+        weigh_scores(0, 0)
+        weigh_y(3, first)
+        weigh_scores(0, 2)
+        bias_scores(0, 1, slice(0, HALF))
+        weigh_target(2, both)
+        bias_scores(0, 3, slice(0, P))
+        bias_scores(0, 3, slice(P, HALF))
         group(nc.scalar.copy, first_grouped[:], xm_raw[0])
-        for s in range(2, PACK):
-            empty_scores(1, s)
+        weigh_scores(1, 0)
+        weigh_scores(1, 2)
+        weigh_scores(1, 3)
 
         g_codes = keep.tile([P, HALF + N], U32, name="g_codes", align_bytes=64)
         g_scales = keep.tile([P, HALF + N], U8, name="g_scales", align_bytes=64)
@@ -213,9 +221,9 @@ def tile_attend_gsq_w_kb_kernel(tc, xT, wT, y, wt, kb, xm, offs, out):
         xm_scales = keep.tile([P, D], U8, name="xm_scales", align_bytes=64)
         xm_codes = keep.tile([P, D], U32, name="xm_codes", align_bytes=64)
         g_first = keep.tile([P, HALF, PACK], BF16, name="g_first", align_bytes=64)[:]
-        g_words = work[:, 8 * HALF + 16 : 10 * HALF + 16]
+        g_words = work[:, 2 * HALF + 16 : 4 * HALF + 16]
         g_second = g_words.bitcast(BF16).rearrange("p (c s) -> p c s", s=PACK)
-        second_grouped = g_second[:, HALF - 8 - P : HALF - 8, :]
+        second_grouped = scores[0][:, 2, :].bitcast(BF16).rearrange("p (c t) -> p c t", t=PACK)
 
         def form_g(engine, h, g_grouped, part):
             engine.tensor_tensor(
@@ -229,9 +237,9 @@ def tile_attend_gsq_w_kb_kernel(tc, xT, wT, y, wt, kb, xm, offs, out):
             cols = slice((h + 1) * HALF, (h + 2) * HALF)
             quantize(g_codes[:, cols], g_scales[:, cols], g_grouped, E5M2X4)
 
-        def gradient_pass(e, cols):
+        def gradient_pass(e, cols, bank):
             feats = slice(e * P, (e + 1) * P)
-            gradient_bank = psum.tile([P, N], F32, name="gradient_bank", tag="bank")
+            gradient_bank = psum.tile([P, N], F32, name="gradient_bank", tag="bank%d" % bank)
             nc.tensor.matmul_mx(
                 out=gradient_bank[:],
                 lhsT=xm_codes[:, feats].bitcast(E4M3X4),
@@ -252,16 +260,15 @@ def tile_attend_gsq_w_kb_kernel(tc, xT, wT, y, wt, kb, xm, offs, out):
         form_g(nc.vector, 0, g_first, slice(P, HALF))
         quantize(xm_codes[:, 0:P], xm_scales[:, 0:P], first_grouped[:], E4M3X4)
         quantize_g(0, g_first)
-        padded_banks = [gradient_pass(0, slice(0, N))]
-        for s in range(2):
-            weigh_target(s + 2, 1, slice(0, HALF))
-            empty_scores(1, s)
+        padded_banks = [gradient_pass(0, slice(0, N), 3)]
+        bias_scores(1, 1, slice(0, HALF))
+        weigh_target(3, second)
         group(nc.scalar.copy, second_grouped, xm_raw[1])
         quantize(xm_codes[:, P : 2 * P], xm_scales[:, P : 2 * P], second_grouped, E4M3X4)
         form_g(nc.vector, 1, g_second, slice(0, G_SPLIT))
         form_g(nc.gpsimd, 1, g_second, slice(G_SPLIT, HALF))
         quantize_g(1, g_second)
-        padded_banks.append(gradient_pass(1, slice(0, N)))
+        padded_banks.append(gradient_pass(1, slice(0, N), 4))
         early_gradients = [
             y_raw[3][:, halves[1]],
             scores[1][:, 1, :],
@@ -269,14 +276,14 @@ def tile_attend_gsq_w_kb_kernel(tc, xT, wT, y, wt, kb, xm, offs, out):
         for e in range(2):
             scatter(e, padded_banks[e][:, HALF:], halves[0], early_gradients[e])
         for e in range(D // P):
-            bank = gradient_pass(e, slice(HALF, HALF + N))
+            bank = gradient_pass(e, slice(HALF, HALF + N), (5, 7, 0, 1)[e])
             if e < 2:
                 scatter(e, bank[:, HALF:], halves[1], keep.tile([P, HALF], F32, name="gradient%d" % e)[:])
             else:
                 scatter(e, bank[:], slice(0, N), keep.tile([P, N], F32, name="gradient%d" % e)[:])
             nc.sync.dma_start(out[e * P : (e + 1) * P, :], windows[e % WINDOWS][:])
             if e == 0:
-                rest_words = work[:, 16 * HALF : 18 * HALF]
+                rest_words = work[:, 11 * HALF : 13 * HALF]
                 rest_grouped = rest_words.bitcast(BF16).rearrange("p (c t) -> p c t", t=PACK)
                 group(nc.scalar.copy, rest_grouped, xm_halves[1][:])
                 quantize(xm_codes[:, 2 * P :], xm_scales[:, 2 * P :], rest_grouped, E4M3X4)

@@ -22,12 +22,25 @@ SUBTRACT = mybir.AluOpType.subtract
 P = 128
 PACK = 4
 BAND = 16
-BANKS = 8
 HALVES = 2
 HALF = N // HALVES
 WINDOWS = 3
-G_SPLIT = 160
+VECTOR_SLOTS = 160
+
 SCORE_BANKS = ((4, 5, 6, 7), (6, 0, 1, 2))
+PADDED_BANKS = (3, 4)
+WHOLE_BANKS = (5, 7, 0, 1)
+
+TARGETS_AT = 0
+X_RAW_AT = 1
+FIRST_SCORES_AT = 7
+FIRST_SCORES_STEP = 4
+SECOND_SCORES_AT = 10
+X_GROUPED_AT = 11
+WORK_CELLS = FIRST_SCORES_AT + PACK * FIRST_SCORES_STEP
+G_SECOND_AT = 2
+XM_REST_AT = 8
+REACH = 16
 
 
 def tile_attend_gsq_w_kb_kernel(tc, xT, wT, y, wt, kb, xm, offs, out):
@@ -58,14 +71,18 @@ def tile_attend_gsq_w_kb_kernel(tc, xT, wT, y, wt, kb, xm, offs, out):
         for t in range(1, PACK):
             nc.sync.dma_start(w_raw[t][:], w_planes[:, t, :])
 
-        work = keep.tile([P, 19 * HALF], F32, name="work", align_bytes=64)
+        work = keep.tile([P, WORK_CELLS * HALF], F32, name="work", align_bytes=64)
 
-        def planes_at(first):
-            return work[:, first * HALF : (first + PACK) * HALF].rearrange("p (s c) -> p s c", s=PACK)
+        def cells(start, count, shift=0):
+            return work[:, start * HALF + shift : (start + count) * HALF + shift]
 
-        target = [planes_at(0), planes_at(4)]
-        scores = [work[:, 7 * HALF :].rearrange("p (s u c) -> p s u c", s=PACK, c=HALF)[:, :, 0, :], planes_at(9)]
-        x_raw = work[:, HALF : HALF + PACK * R].rearrange("p (t r) -> p t r", t=PACK)
+        def grouped_view(words):
+            return words.bitcast(BF16).rearrange("p (c t) -> p c t", t=PACK)
+
+        targets = cells(TARGETS_AT, HALVES * PACK).rearrange("p (h s c) -> p h s c", h=HALVES, s=PACK)
+        spaced = cells(FIRST_SCORES_AT, PACK * FIRST_SCORES_STEP).rearrange("p (s u c) -> p s u c", s=PACK, c=HALF)
+        scores = [spaced[:, :, 0, :], cells(SECOND_SCORES_AT, PACK).rearrange("p (s c) -> p s c", s=PACK)]
+        x_raw = cells(X_RAW_AT, PACK * R // HALF).rearrange("p (t r) -> p t r", t=PACK)
         nc.sync.dma_start(x_raw, xT[0].rearrange("(p t) r -> p t r", t=PACK))
 
         y_planes = y[0].rearrange("(p t) n -> p t n", t=PACK)
@@ -78,7 +95,6 @@ def tile_attend_gsq_w_kb_kernel(tc, xT, wT, y, wt, kb, xm, offs, out):
         xm_halves = [keep.tile([P, PACK, D // 2], F32, name="xm_half%d" % v) for v in range(2)]
         for v in range(2):
             nc.sync.dma_start(xm_halves[v][:], xm_planes[:, :, v * (D // 2) : (v + 1) * (D // 2)])
-        xm_raw = [xm_halves[e // 2][:, :, (e % 2) * P : (e % 2 + 1) * P] for e in range(D // P)]
 
         identity = keep.tile([P, P], F32, name="identity", tag="identity_then_window")
         make_identity(nc, identity[:])
@@ -98,7 +114,7 @@ def tile_attend_gsq_w_kb_kernel(tc, xT, wT, y, wt, kb, xm, offs, out):
         windows.append(keep.tile([P, T], F32, name="last_window", tag="identity_then_window"))
         nc.gpsimd.memset(windows[-1][:].bitcast(I32), 0)
 
-        kb_listed = keep.tile([P, N], F32, name="kb_listed", tag="kb_x_target", align_bytes=64)
+        kb_listed = keep.tile([P, N], F32, name="kb_listed", tag="kb_then_x", align_bytes=64)
         nc.vector.tensor_copy(kb_listed[:], kb_window[:].indirect(offsets[:]))
         kb_weighted = keep.tile([P, PACK, HALVES, HALF], F32, name="kb_weighted")
         for t in range(PACK):
@@ -134,26 +150,20 @@ def tile_attend_gsq_w_kb_kernel(tc, xT, wT, y, wt, kb, xm, offs, out):
             quantize(w_codes[h], w_scales[:, slots], w_grouped[h][:], E4M3X4)
 
         x_grouped = [
-            keep.tile([P, 2, P, PACK], BF16, name="x_grouped0", tag="kb_x_target", align_bytes=64)[:],
-            work[:, 10 * HALF : 12 * HALF].bitcast(BF16).rearrange("p (s m t) -> p s m t", s=2, t=PACK),
+            keep.tile([P, 2, P, PACK], BF16, name="x_grouped0", tag="kb_then_x", align_bytes=64)[:],
+            cells(X_GROUPED_AT, 2).bitcast(BF16).rearrange("p (s m t) -> p s m t", s=2, t=PACK),
         ]
-
-        def deal_x(copy, u, m):
+        for u, copy in enumerate((nc.vector.tensor_copy, nc.scalar.copy)):
             copy(
-                x_grouped[u].rearrange("p s m t -> p m t s")[:, m],
-                x_raw.rearrange("p t (m s) -> p m t s", s=PACK)[:, m, :, 2 * u : 2 * u + 2],
+                x_grouped[u].rearrange("p s m t -> p m t s"),
+                x_raw.rearrange("p t (m s) -> p m t s", s=PACK)[:, :, :, 2 * u : 2 * u + 2],
             )
-
-        deal_x(nc.vector.tensor_copy, 0, slice(0, P))
-        deal_x(nc.scalar.copy, 1, slice(0, P))
         x_codes = keep.tile([P, R], U32, name="x_codes", align_bytes=64)
         x_scales = keep.tile([P, R], U8, name="x_scales", align_bytes=64)
         for u in range(2):
             cols = slice(u * 2 * P, (u + 1) * 2 * P)
             quantize(x_codes[:, cols], x_scales[:, cols], x_grouped[u].rearrange("p s m t -> p (s m) t"), E4M3X4)
 
-
-        targets = work[:, 0 : 8 * HALF].rearrange("p (h s c) -> p s h c", h=HALVES, s=PACK)
         first, second, both = slice(0, 1), slice(1, 2), slice(0, 2)
 
         def y_part(s, hs):
@@ -161,17 +171,17 @@ def tile_attend_gsq_w_kb_kernel(tc, xT, wT, y, wt, kb, xm, offs, out):
 
         def weigh_target(s, hs):
             nc.vector.scalar_tensor_tensor(
-                targets[:, s, hs], y_part(s, hs), row_weight[:, s : s + 1], kb_weighted[:, s, hs], MULT, SUBTRACT
+                targets[:, hs, s], y_part(s, hs), row_weight[:, s : s + 1], kb_weighted[:, s, hs], MULT, SUBTRACT
             )
 
         def weigh_y(s, hs):
-            nc.scalar.activation(targets[:, s, hs], y_part(s, hs), COPY, scale=row_weight[:, s : s + 1])
+            nc.scalar.activation(targets[:, hs, s], y_part(s, hs), COPY, scale=row_weight[:, s : s + 1])
 
         weigh_target(0, first)
         weigh_target(0, second)
         weigh_y(1, both)
 
-        first_grouped = keep.tile([P, P, PACK], BF16, name="first_grouped", tag="w_then_xm", align_bytes=64)
+        xm_first = keep.tile([P, P, PACK], BF16, name="xm_first", tag="w_then_xm", align_bytes=64)
         score_banks = {}
 
         def weigh_scores(h, s):
@@ -208,7 +218,7 @@ def tile_attend_gsq_w_kb_kernel(tc, xT, wT, y, wt, kb, xm, offs, out):
         weigh_target(2, both)
         bias_scores(0, 3, slice(0, P))
         bias_scores(0, 3, slice(P, HALF))
-        group(nc.scalar.copy, first_grouped[:], xm_raw[0])
+        group(nc.scalar.copy, xm_first[:], xm_halves[0][:, :, 0:P])
         weigh_scores(1, 0)
         weigh_scores(1, 2)
         weigh_scores(1, 3)
@@ -221,15 +231,15 @@ def tile_attend_gsq_w_kb_kernel(tc, xT, wT, y, wt, kb, xm, offs, out):
         xm_scales = keep.tile([P, D], U8, name="xm_scales", align_bytes=64)
         xm_codes = keep.tile([P, D], U32, name="xm_codes", align_bytes=64)
         g_first = keep.tile([P, HALF, PACK], BF16, name="g_first", align_bytes=64)[:]
-        g_words = work[:, 2 * HALF + 16 : 4 * HALF + 16]
-        g_second = g_words.bitcast(BF16).rearrange("p (c s) -> p c s", s=PACK)
-        second_grouped = scores[0][:, 2, :].bitcast(BF16).rearrange("p (c t) -> p c t", t=PACK)
+        g_second = grouped_view(cells(G_SECOND_AT, 2, REACH))
+        xm_second = grouped_view(scores[0][:, 2, :])
+        xm_rest = grouped_view(cells(XM_REST_AT, 2, REACH))
 
         def form_g(engine, h, g_grouped, part):
             engine.tensor_tensor(
                 g_grouped[:, part, :].rearrange("p (c i) s -> p c s i", i=4),
                 scores[h][:, :, part].rearrange("p s (c i) -> p c s i", i=4),
-                target[h][:, :, part].rearrange("p s (c i) -> p c s i", i=4),
+                targets[:, h, :, part].rearrange("p s (c i) -> p c s i", i=4),
                 SUBTRACT,
             )
 
@@ -258,32 +268,27 @@ def tile_attend_gsq_w_kb_kernel(tc, xT, wT, y, wt, kb, xm, offs, out):
 
         form_g(nc.vector, 0, g_first, slice(0, P))
         form_g(nc.vector, 0, g_first, slice(P, HALF))
-        quantize(xm_codes[:, 0:P], xm_scales[:, 0:P], first_grouped[:], E4M3X4)
+        quantize(xm_codes[:, 0:P], xm_scales[:, 0:P], xm_first[:], E4M3X4)
         quantize_g(0, g_first)
-        padded_banks = [gradient_pass(0, slice(0, N), 3)]
+        padded_banks = [gradient_pass(0, slice(0, N), PADDED_BANKS[0])]
         bias_scores(1, 1, slice(0, HALF))
         weigh_target(3, second)
-        group(nc.scalar.copy, second_grouped, xm_raw[1])
-        quantize(xm_codes[:, P : 2 * P], xm_scales[:, P : 2 * P], second_grouped, E4M3X4)
-        form_g(nc.vector, 1, g_second, slice(0, G_SPLIT))
-        form_g(nc.gpsimd, 1, g_second, slice(G_SPLIT, HALF))
+        group(nc.scalar.copy, xm_second, xm_halves[0][:, :, P:])
+        quantize(xm_codes[:, P : 2 * P], xm_scales[:, P : 2 * P], xm_second, E4M3X4)
+        form_g(nc.vector, 1, g_second, slice(0, VECTOR_SLOTS))
+        form_g(nc.gpsimd, 1, g_second, slice(VECTOR_SLOTS, HALF))
         quantize_g(1, g_second)
-        padded_banks.append(gradient_pass(1, slice(0, N), 4))
-        early_gradients = [
-            y_raw[3][:, halves[1]],
-            scores[1][:, 1, :],
-        ]
-        for e in range(2):
-            scatter(e, padded_banks[e][:, HALF:], halves[0], early_gradients[e])
+        padded_banks.append(gradient_pass(1, slice(0, N), PADDED_BANKS[1]))
+        padded_gradients = [y_raw[3][:, halves[1]], scores[1][:, 1, :]]
+        for e, bank in enumerate(padded_banks):
+            scatter(e, bank[:, HALF:], halves[0], padded_gradients[e])
         for e in range(D // P):
-            bank = gradient_pass(e, slice(HALF, HALF + N), (5, 7, 0, 1)[e])
-            if e < 2:
+            bank = gradient_pass(e, slice(HALF, HALF + N), WHOLE_BANKS[e])
+            if e < len(padded_banks):
                 scatter(e, bank[:, HALF:], halves[1], keep.tile([P, HALF], F32, name="gradient%d" % e)[:])
             else:
                 scatter(e, bank[:], slice(0, N), keep.tile([P, N], F32, name="gradient%d" % e)[:])
             nc.sync.dma_start(out[e * P : (e + 1) * P, :], windows[e % WINDOWS][:])
             if e == 0:
-                rest_words = work[:, 11 * HALF : 13 * HALF]
-                rest_grouped = rest_words.bitcast(BF16).rearrange("p (c t) -> p c t", t=PACK)
-                group(nc.scalar.copy, rest_grouped, xm_halves[1][:])
-                quantize(xm_codes[:, 2 * P :], xm_scales[:, 2 * P :], rest_grouped, E4M3X4)
+                group(nc.scalar.copy, xm_rest, xm_halves[1][:])
+                quantize(xm_codes[:, 2 * P :], xm_scales[:, 2 * P :], xm_rest, E4M3X4)

@@ -16,47 +16,45 @@ E4M3X4 = mybir.dt.float8_e4m3fn_x4
 E5M2X4 = mybir.dt.float8_e5m2_x4
 COPY = mybir.ActivationFunctionType.Copy
 MULT = mybir.AluOpType.mult
-ADD = mybir.AluOpType.add
 SUBTRACT = mybir.AluOpType.subtract
 
 P = 128
 PACK = 4
 BAND = 16
-HALVES = 2
-HALF = N // HALVES
-WINDOWS = 3
-VECTOR_SLOTS = 160
-
-SCORE_BANKS = ((4, 5, 6, 7), (6, 0, 1, 2))
-PADDED_BANKS = (3, 4)
-WHOLE_BANKS = (5, 7, 0, 1)
+HALF = N // 2
+FIRST, SECOND = slice(0, HALF), slice(HALF, N)
 
 TARGETS_AT = 0
-X_RAW_AT = 1
+X_GROUPED_WORD = 3 * HALF // 2
+X_GROUPED_STEP = 7 * HALF // 2
 FIRST_SCORES_AT = 7
-FIRST_SCORES_STEP = 4
-SECOND_SCORES_AT = 10
-X_GROUPED_AT = 11
-WORK_CELLS = FIRST_SCORES_AT + PACK * FIRST_SCORES_STEP
-G_SECOND_AT = 2
+G_AT = 15
 XM_REST_AT = 8
-REACH = 16
+WORK_CELLS = 19
 
 
 def tile_attend_gsq_w_kb_kernel(tc, xT, wT, y, wt, kb, xm, offs, out):
     nc = tc.nc
-    halves = [slice(h * HALF, (h + 1) * HALF) for h in range(HALVES)]
+    halves = [FIRST, SECOND]
 
     with ExitStack() as ctx:
         keep = ctx.enter_context(tc.tile_pool(name="keep", bufs=1))
         shared = ctx.enter_context(tc.tile_pool(name="shared", bufs=1))
+        cleared = ctx.enter_context(tc.tile_pool(name="cleared", bufs=1))
+        late = ctx.enter_context(tc.tile_pool(name="late", bufs=1))
         psum = ctx.enter_context(tc.psum_pool(name="psum", bufs=1))
 
         def quantize(codes, scales, grouped, dtype):
             nc.vector.quantize_mx(out=codes.bitcast(dtype), scales=scales, in_=grouped.rearrange("p c t -> p (c t)"))
 
-        def group(copy, grouped, planes):
-            copy(grouped.rearrange("p (c i) t -> p c t i", i=4), planes.rearrange("p t (c i) -> p c t i", i=4))
+        def by_fours(grouped, planes):
+            return (
+                grouped.rearrange("p (c i) t -> p c t i", i=4),
+                planes.rearrange("p t (c i) -> p c t i", i=4),
+            )
+
+        def listed(slots):
+            return offsets[:, slots.start // BAND : slots.stop // BAND]
 
         kb_columns = keep.tile([P, T // P], F32, name="kb_columns")
         nc.sync.dma_start(kb_columns[:], kb[0].rearrange("(p c) -> p c", p=P))
@@ -71,34 +69,37 @@ def tile_attend_gsq_w_kb_kernel(tc, xT, wT, y, wt, kb, xm, offs, out):
         for t in range(1, PACK):
             nc.sync.dma_start(w_raw[t][:], w_planes[:, t, :])
 
-        work = keep.tile([P, WORK_CELLS * HALF], F32, name="work", align_bytes=64)
+        work = shared.tile([P, WORK_CELLS * HALF], F32, name="work", offset=0, align_bytes=64)
 
-        def cells(start, count, shift=0):
-            return work[:, start * HALF + shift : (start + count) * HALF + shift]
+        def cells(start, count):
+            return work[:, start * HALF : (start + count) * HALF]
 
         def grouped_view(words):
             return words.bitcast(BF16).rearrange("p (c t) -> p c t", t=PACK)
 
-        targets = cells(TARGETS_AT, HALVES * PACK).rearrange("p (h s c) -> p h s c", h=HALVES, s=PACK)
-        spaced = cells(FIRST_SCORES_AT, PACK * FIRST_SCORES_STEP).rearrange("p (s u c) -> p s u c", s=PACK, c=HALF)
-        scores = [spaced[:, :, 0, :], cells(SECOND_SCORES_AT, PACK).rearrange("p (s c) -> p s c", s=PACK)]
-        x_raw = cells(X_RAW_AT, PACK * R // HALF).rearrange("p (t r) -> p t r", t=PACK)
-        nc.sync.dma_start(x_raw, xT[0].rearrange("(p t) r -> p t r", t=PACK))
+        targets = cells(TARGETS_AT, 2 * PACK).rearrange("p (s h c) -> p h s c", h=2, s=PACK)
+        scores = cells(FIRST_SCORES_AT, 2 * PACK).rearrange("p (h s c) -> p h s c", h=2, s=PACK)
+        x_planes = xT[0].rearrange("(p t) r -> p t r", t=PACK)
+        x_pairs = [keep.tile([P, 2, R], F32, name="x_pair%d" % u) for u in range(2)]
+        for u in range(2):
+            nc.sync.dma_start(x_pairs[u][:], x_planes[:, 2 * u : 2 * u + 2, :])
 
         y_planes = y[0].rearrange("(p t) n -> p t n", t=PACK)
         y_pairs = [keep.tile([P, 2, N], F32, name="y_pair%d" % u) for u in range(2)]
         for u in range(2):
             nc.sync.dma_start(y_pairs[u][:], y_planes[:, 2 * u : 2 * u + 2, :])
-        y_raw = [y_pairs[t // 2][:, t % 2, :] for t in range(PACK)]
 
         xm_planes = xm[0].rearrange("(p t) d -> p t d", t=PACK)
-        xm_halves = [keep.tile([P, PACK, D // 2], F32, name="xm_half%d" % v) for v in range(2)]
+        xm_halves = [
+            keep.tile([P, PACK, D // 2], F32, name="xm_half0"),
+            late.tile([P, PACK, D // 2], F32, name="xm_half1", offset=1024, align_bytes=64),
+        ]
         for v in range(2):
             nc.sync.dma_start(xm_halves[v][:], xm_planes[:, :, v * (D // 2) : (v + 1) * (D // 2)])
 
-        identity = keep.tile([P, P], F32, name="identity", tag="identity_then_window")
+        identity = cleared.tile([P, P], F32, name="identity", offset=4 * T - 256)
         make_identity(nc, identity[:])
-        windows = [keep.tile([P, T], F32, name="window%d" % w) for w in range(WINDOWS - 1)]
+        windows = [keep.tile([P, T], F32, name="window%d" % w) for w in range(2)]
         for window in windows:
             nc.vector.memset(window[:].bitcast(I32), 0)
         kb_window = shared.tile([P, T], F32, name="kb_window", offset=0, align_bytes=64)
@@ -111,184 +112,178 @@ def tile_attend_gsq_w_kb_kernel(tc, xT, wT, y, wt, kb, xm, offs, out):
                 nc.tensor.transpose(spread[:, c, :], column.to_broadcast([P, P]), identity[:])
             nc.scalar.copy(kb_items[:, :, c0 : c0 + turns_per_bank], spread[:].rearrange("p c n -> p n c"))
 
-        windows.append(keep.tile([P, T], F32, name="last_window", tag="identity_then_window"))
-        nc.gpsimd.memset(windows[-1][:].bitcast(I32), 0)
+        for w in range(2):
+            windows.append(cleared.tile([P, T], F32, name="window%d" % (2 + w), offset=4 * T * w))
+            nc.gpsimd.memset(windows[-1][:].bitcast(I32), 0)
 
-        kb_listed = keep.tile([P, N], F32, name="kb_listed", tag="kb_then_x", align_bytes=64)
+        kb_listed = keep.tile([P, N], F32, name="kb_listed", align_bytes=64)
         nc.vector.tensor_copy(kb_listed[:], kb_window[:].indirect(offsets[:]))
-        kb_weighted = keep.tile([P, PACK, HALVES, HALF], F32, name="kb_weighted")
+        kb_weighted = keep.tile([P, PACK, 2, HALF], F32, name="kb_weighted")
         for t in range(PACK):
             nc.scalar.activation(
                 kb_weighted[:, t].rearrange("p h c -> p (h c)"), kb_listed[:], COPY, scale=row_weight[:, t : t + 1]
             )
 
-        w_listed = [
-            shared.tile([P, 2, N], BF16, name="w_listed0", offset=6144, align_bytes=64),
-            shared.tile([P, 2, N], BF16, name="w_listed1", offset=0, align_bytes=64),
-        ]
+        x_spaced = work[:, X_GROUPED_WORD : X_GROUPED_WORD + 2 * X_GROUPED_STEP].bitcast(BF16)
+        x_spaced = x_spaced.rearrange("p (v z) -> p v z", v=2)
+        w_listed = [x_spaced[:, h, 0 : 3 * HALF].rearrange("p (r c) -> p r c", r=3) for h in range(2)]
         w_grouped = [
-            shared.tile([P, HALF, PACK], BF16, name="w_grouped%d" % h, offset=2048 * (h + 1), align_bytes=64)
-            for h in range(HALVES)
+            keep.tile([P, HALF, PACK], BF16, name="w_grouped%d" % h, align_bytes=64) for h in range(2)
         ]
+        w_row = (1, 2, 0, 1)
 
         def group_pair(copy, u, h):
-            copy(w_grouped[h][:, :, 2 * u : 2 * u + 2], w_listed[u][:, :, halves[h]].rearrange("p t c -> p c t"))
+            pair = w_listed[h][:, w_row[2 * u] : w_row[2 * u] + 2]
+            copy(w_grouped[h][:, :, 2 * u : 2 * u + 2], pair.rearrange("p t c -> p c t"))
 
-        for t in range(PACK - 1):
-            nc.vector.tensor_copy(w_listed[t // 2][:, t % 2, :], w_raw[t][:].indirect(offsets[:]))
-        for h in range(HALVES):
+        def gather(t, h):
+            nc.vector.tensor_copy(w_listed[h][:, w_row[t]], w_raw[t][:].indirect(listed(halves[h])))
+
+        for t in range(2):
+            for h in range(2):
+                gather(t, h)
+        for h in range(2):
             group_pair(nc.scalar.copy, 0, h)
-        for slots in halves:
-            listed = offsets[:, slots.start // BAND : slots.stop // BAND]
-            nc.vector.tensor_copy(w_listed[1][:, 1, slots], w_raw[PACK - 1][:].indirect(listed))
-        w_codes = [keep.tile([P, HALF], U32, name="w_codes0", tag="w_then_xm", align_bytes=64)[:]]
-        w_scales = keep.tile([P, N], U8, name="w_scales", align_bytes=64)
-        group_pair(nc.scalar.copy, 1, 1)
+        for h in range(2):
+            gather(2, h)
+        gather(3, 0)
+        nc.scalar.activation(w_listed[1][:, w_row[3]], w_raw[3][:].indirect(listed(SECOND)), COPY)
         group_pair(nc.vector.tensor_copy, 1, 0)
-        w_codes.append(keep.tile([P, HALF], U32, name="w_codes1", align_bytes=64)[:])
-        for h, slots in enumerate(halves):
-            quantize(w_codes[h], w_scales[:, slots], w_grouped[h][:], E4M3X4)
-
-        x_grouped = [
-            keep.tile([P, 2, P, PACK], BF16, name="x_grouped0", tag="kb_then_x", align_bytes=64)[:],
-            cells(X_GROUPED_AT, 2).bitcast(BF16).rearrange("p (s m t) -> p s m t", s=2, t=PACK),
+        group_pair(nc.scalar.copy, 1, 1)
+        w_codes = [
+            late.tile([P, HALF], U32, name="w_codes0", offset=0, align_bytes=64),
+            keep.tile([P, HALF], U32, name="w_codes1", align_bytes=64),
         ]
-        for u, copy in enumerate((nc.vector.tensor_copy, nc.scalar.copy)):
-            copy(
-                x_grouped[u].rearrange("p s m t -> p m t s"),
-                x_raw.rearrange("p t (m s) -> p m t s", s=PACK)[:, :, :, 2 * u : 2 * u + 2],
-            )
+        w_scales = keep.tile([P, N], U8, name="w_scales", align_bytes=64)
+        quantize(w_codes[0][:], w_scales[:, FIRST], w_grouped[0][:], E4M3X4)
+
+        x_grouped = x_spaced[:, :, 0 : 2 * P * PACK].rearrange("p v (s m t) -> p v s m t", s=2, t=PACK)
+        for u in range(2):
+            rows = x_pairs[u][:].rearrange("p t (m v s) -> p v m t s", v=2, s=2)
+            for v, copy in enumerate((nc.vector.tensor_copy, nc.scalar.copy)):
+                copy(x_grouped[:, v, :, :, 2 * u : 2 * u + 2].rearrange("p s m t -> p m t s"), rows[:, v])
+        quantize(w_codes[1][:], w_scales[:, SECOND], w_grouped[1][:], E4M3X4)
         x_codes = keep.tile([P, R], U32, name="x_codes", align_bytes=64)
         x_scales = keep.tile([P, R], U8, name="x_scales", align_bytes=64)
-        for u in range(2):
-            cols = slice(u * 2 * P, (u + 1) * 2 * P)
-            quantize(x_codes[:, cols], x_scales[:, cols], x_grouped[u].rearrange("p s m t -> p (s m) t"), E4M3X4)
-
-        first, second, both = slice(0, 1), slice(1, 2), slice(0, 2)
-
-        def y_part(s, hs):
-            return y_raw[s].rearrange("p (h c) -> p h c", h=HALVES)[:, hs]
-
-        def weigh_target(s, hs):
-            nc.vector.scalar_tensor_tensor(
-                targets[:, hs, s], y_part(s, hs), row_weight[:, s : s + 1], kb_weighted[:, s, hs], MULT, SUBTRACT
-            )
-
-        def weigh_y(s, hs):
-            nc.scalar.activation(targets[:, hs, s], y_part(s, hs), COPY, scale=row_weight[:, s : s + 1])
-
-        weigh_target(0, first)
-        weigh_target(0, second)
-        weigh_y(1, both)
-
-        xm_first = keep.tile([P, P, PACK], BF16, name="xm_first", tag="w_then_xm", align_bytes=64)
-        score_banks = {}
+        for v in range(2):
+            cols = slice(2 * P * v, 2 * P * (v + 1))
+            quantize(x_codes[:, cols], x_scales[:, cols], x_grouped[:, v].rearrange("p s m t -> p (s m) t"), E4M3X4)
 
         def weigh_scores(h, s):
-            nc.scalar.activation(scores[h][:, s, :], score_banks[h, s][:], COPY, scale=row_weight[:, s : s + 1])
-
-        def bias_scores(h, s, part):
-            nc.vector.scalar_tensor_tensor(
-                scores[h][:, s, part],
-                score_banks[h, s][:, part],
-                row_weight[:, s : s + 1],
-                kb_weighted[:, s, h, part],
-                MULT,
-                ADD,
+            rows = slice(s * P, (s + 1) * P)
+            bank = psum.tile([P, HALF], F32, name="score_bank", tag="bank%d" % ((4 + 4 * h + s) % 8))
+            nc.tensor.matmul_mx(
+                out=bank[:],
+                lhsT=x_codes[:, rows].bitcast(E4M3X4),
+                lhsT_scale=x_scales[:, rows],
+                rhs=w_codes[h][:].bitcast(E4M3X4),
+                rhs_scale=w_scales[:, halves[h]],
+                start=True,
+                stop=True,
             )
+            nc.scalar.activation(scores[:, h, s], bank[:], COPY, scale=row_weight[:, s : s + 1])
 
-        for h, slots in enumerate(halves):
-            for s in range(PACK):
-                rows = slice(s * P, (s + 1) * P)
-                score_bank = psum.tile([P, HALF], F32, name="score_bank", tag="bank%d" % SCORE_BANKS[h][s])
-                score_banks[h, s] = score_bank
-                nc.tensor.matmul_mx(
-                    out=score_bank[:],
-                    lhsT=x_codes[:, rows].bitcast(E4M3X4),
-                    lhsT_scale=x_scales[:, rows],
-                    rhs=w_codes[h].bitcast(E4M3X4),
-                    rhs_scale=w_scales[:, slots],
-                    start=True,
-                    stop=True,
-                )
-        weigh_scores(0, 0)
-        weigh_y(3, first)
-        weigh_scores(0, 2)
-        bias_scores(0, 1, slice(0, HALF))
-        weigh_target(2, both)
-        bias_scores(0, 3, slice(0, P))
-        bias_scores(0, 3, slice(P, HALF))
-        group(nc.scalar.copy, xm_first[:], xm_halves[0][:, :, 0:P])
-        weigh_scores(1, 0)
-        weigh_scores(1, 2)
-        weigh_scores(1, 3)
-
-        g_codes = keep.tile([P, HALF + N], U32, name="g_codes", align_bytes=64)
-        g_scales = keep.tile([P, HALF + N], U8, name="g_scales", align_bytes=64)
-        nc.gpsimd.memset(g_codes[:, 0:HALF], 0)
-        nc.gpsimd.memset(g_scales[:, 0:HALF], 0)
-
-        xm_scales = keep.tile([P, D], U8, name="xm_scales", align_bytes=64)
-        xm_codes = keep.tile([P, D], U32, name="xm_codes", align_bytes=64)
-        g_first = keep.tile([P, HALF, PACK], BF16, name="g_first", align_bytes=64)[:]
-        g_second = grouped_view(cells(G_SECOND_AT, 2, REACH))
-        xm_second = grouped_view(scores[0][:, 2, :])
-        xm_rest = grouped_view(cells(XM_REST_AT, 2, REACH))
-
-        def form_g(engine, h, g_grouped, part):
-            engine.tensor_tensor(
-                g_grouped[:, part, :].rearrange("p (c i) s -> p c s i", i=4),
-                scores[h][:, :, part].rearrange("p s (c i) -> p c s i", i=4),
-                targets[:, h, :, part].rearrange("p s (c i) -> p c s i", i=4),
+        def weigh_target(s, hs):
+            y_plane = y_pairs[s // 2][:, s % 2, :].rearrange("p (h c) -> p h c", h=2)
+            nc.vector.scalar_tensor_tensor(
+                targets[:, hs, s],
+                y_plane[:, hs],
+                row_weight[:, s : s + 1],
+                kb_weighted[:, s, hs],
+                MULT,
                 SUBTRACT,
             )
 
-        def quantize_g(h, g_grouped):
-            cols = slice((h + 1) * HALF, (h + 2) * HALF)
-            quantize(g_codes[:, cols], g_scales[:, cols], g_grouped, E5M2X4)
+        first, second, both = slice(0, 1), slice(1, 2), slice(0, 2)
+        xm_first = late.tile([P, P, PACK], BF16, name="xm_first", offset=0, align_bytes=64)
+        for s in range(PACK):
+            weigh_scores(0, s)
+        for s in range(PACK):
+            if s == 2:
+                nc.scalar.copy(*by_fours(xm_first[:], xm_halves[0][:, :, 0:P]))
+            weigh_scores(1, s)
+        weigh_target(0, both)
+        weigh_target(1, first)
+        weigh_target(2, both)
+        weigh_target(3, first)
+        weigh_target(1, second)
 
-        def gradient_pass(e, cols, bank):
+        g_codes = keep.tile([P, N], U32, name="g_codes", align_bytes=64)
+        g_scales = keep.tile([P, N], U8, name="g_scales", align_bytes=64)
+        xm_scales = keep.tile([P, D], U8, name="xm_scales", align_bytes=64)
+        xm_codes = keep.tile([P, D], U32, name="xm_codes", align_bytes=64)
+        g_grouped = grouped_view(cells(G_AT, 4))
+        xm_second = grouped_view(scores[:, 0, 1])
+        xm_rest = grouped_view(cells(XM_REST_AT, 2))
+
+        def form_g(h):
+            nc.vector.tensor_tensor(
+                g_grouped[:, halves[h], :].rearrange("p (c i) s -> p c s i", i=4),
+                scores[:, h].rearrange("p s (c i) -> p c s i", i=4),
+                targets[:, h].rearrange("p s (c i) -> p c s i", i=4),
+                SUBTRACT,
+            )
+
+        def quantize_g(slots):
+            quantize(g_codes[:, slots], g_scales[:, slots], g_grouped[:, slots], E5M2X4)
+
+        def quantize_xm(feats, grouped):
+            quantize(xm_codes[:, feats], xm_scales[:, feats], grouped, E4M3X4)
+
+        def gradient_pass(e, slots, bank):
             feats = slice(e * P, (e + 1) * P)
-            gradient_bank = psum.tile([P, N], F32, name="gradient_bank", tag="bank%d" % bank)
+            gradient_bank = psum.tile([P, slots.stop - slots.start], F32, name="gradient_bank", tag="bank%d" % bank)
             nc.tensor.matmul_mx(
                 out=gradient_bank[:],
                 lhsT=xm_codes[:, feats].bitcast(E4M3X4),
                 lhsT_scale=xm_scales[:, feats],
-                rhs=g_codes[:, cols].bitcast(E5M2X4),
-                rhs_scale=g_scales[:, cols],
+                rhs=g_codes[:, slots].bitcast(E5M2X4),
+                rhs_scale=g_scales[:, slots],
                 start=True,
                 stop=True,
             )
-            return gradient_bank
+            return gradient_bank[:]
 
-        def scatter(e, bank_cols, slots, gradient):
-            nc.scalar.copy(gradient, bank_cols)
-            listed = offsets[:, slots.start // BAND : slots.stop // BAND]
-            nc.vector.tensor_copy(windows[e % WINDOWS][:].indirect(listed), gradient)
+        def scalar_scatter(e, slots, gradient):
+            nc.scalar.activation(windows[e][:].indirect(listed(slots)), gradient, COPY)
 
-        form_g(nc.vector, 0, g_first, slice(0, P))
-        form_g(nc.vector, 0, g_first, slice(P, HALF))
-        quantize(xm_codes[:, 0:P], xm_scales[:, 0:P], xm_first[:], E4M3X4)
-        quantize_g(0, g_first)
-        padded_banks = [gradient_pass(0, slice(0, N), PADDED_BANKS[0])]
-        bias_scores(1, 1, slice(0, HALF))
+        def store(e):
+            nc.sync.dma_start(out[e * P : (e + 1) * P, :], windows[e][:])
+
+        form_g(0)
+        quantize_xm(slice(0, P), xm_first[:])
         weigh_target(3, second)
-        group(nc.scalar.copy, xm_second, xm_halves[0][:, :, P:])
-        quantize(xm_codes[:, P : 2 * P], xm_scales[:, P : 2 * P], xm_second, E4M3X4)
-        form_g(nc.vector, 1, g_second, slice(0, VECTOR_SLOTS))
-        form_g(nc.gpsimd, 1, g_second, slice(VECTOR_SLOTS, HALF))
-        quantize_g(1, g_second)
-        padded_banks.append(gradient_pass(1, slice(0, N), PADDED_BANKS[1]))
-        padded_gradients = [y_raw[3][:, halves[1]], scores[1][:, 1, :]]
-        for e, bank in enumerate(padded_banks):
-            scatter(e, bank[:, HALF:], halves[0], padded_gradients[e])
-        for e in range(D // P):
-            bank = gradient_pass(e, slice(HALF, HALF + N), WHOLE_BANKS[e])
-            if e < len(padded_banks):
-                scatter(e, bank[:, HALF:], halves[1], keep.tile([P, HALF], F32, name="gradient%d" % e)[:])
-            else:
-                scatter(e, bank[:], slice(0, N), keep.tile([P, N], F32, name="gradient%d" % e)[:])
-            nc.sync.dma_start(out[e * P : (e + 1) * P, :], windows[e % WINDOWS][:])
-            if e == 0:
-                group(nc.scalar.copy, xm_rest, xm_halves[1][:])
-                quantize(xm_codes[:, 2 * P :], xm_scales[:, 2 * P :], xm_rest, E4M3X4)
+        quantize_g(FIRST)
+        nc.scalar.copy(*by_fours(xm_second, xm_halves[0][:, :, P:]))
+        gradient_a = keep.tile([P, HALF], F32, name="gradient_a")
+        nc.scalar.copy(gradient_a[:], gradient_pass(0, FIRST, 4))
+        scalar_scatter(0, FIRST, gradient_a[:])
+
+        form_g(1)
+        quantize_xm(slice(P, 2 * P), xm_second)
+        quantize_g(SECOND)
+        nc.vector.tensor_copy(*by_fours(xm_rest, xm_halves[1][:]))
+
+        gradient_b = keep.tile([P, HALF], F32, name="gradient_b")
+        nc.vector.tensor_copy(gradient_b[:], gradient_pass(0, SECOND, 5))
+        gradient_1 = late.tile([P, N], F32, name="gradient_1", offset=1024, align_bytes=64)
+        for h in range(2):
+            nc.scalar.copy(gradient_1[:, halves[h]], gradient_pass(1, halves[h], (6, 1)[h]))
+        quantize_xm(slice(2 * P, D), xm_rest)
+        nc.vector.tensor_copy(windows[0][:].indirect(listed(SECOND)), gradient_b[:])
+        store(0)
+        for slots in halves:
+            scalar_scatter(1, slots, gradient_1[:, slots])
+        store(1)
+
+        gradient_2 = keep.tile([P, N], F32, name="gradient_2")
+        nc.vector.tensor_copy(gradient_2[:], gradient_pass(2, slice(0, N), 7))
+        nc.vector.tensor_copy(windows[2][:].indirect(offsets[:]), gradient_2[:])
+        store(2)
+
+        gradient_3 = keep.tile([P, N], F32, name="gradient_3")
+        for h in range(2):
+            nc.scalar.copy(gradient_3[:, halves[h]], gradient_pass(3, halves[h], (0, 2)[h]))
+        for slots in halves:
+            scalar_scatter(3, slots, gradient_3[:, slots])
+        store(3)

@@ -264,26 +264,26 @@ def tile_attend_gsq_w_kb_kernel(tc, xT, wT, y, wt, kb, xm, offs, out):
         quantize_g(SECOND)
         nc.vector.tensor_copy(*by_fours(xm_rest, xm_halves[1][:]))
 
-        gradient_b = keep.tile([P, HALF], F32, name="gradient_b")
-        nc.vector.tensor_copy(gradient_b[:], gradient_pass(0, SECOND, 5))
+        late_halves = [keep.tile([P, HALF], F32, name="late_half%d" % e) for e in range(PACK)]
+        nc.vector.tensor_copy(late_halves[0][:], gradient_pass(0, SECOND, 5))
         gradient_1 = late.tile([P, N], F32, name="gradient_1", offset=1024, align_bytes=64)
         for h in range(2):
             nc.scalar.copy(gradient_1[:, halves[h]], gradient_pass(1, halves[h], (6, 1)[h]))
         quantize_xm(slice(2 * P, D), xm_rest)
-        nc.vector.tensor_copy(windows[0][:].indirect(listed(SECOND)), gradient_b[:])
-        store(0)
-        for slots in halves:
-            scalar_scatter(1, slots, gradient_1[:, slots])
-        store(1)
 
-        gradient_2 = keep.tile([P, N], F32, name="gradient_2")
-        nc.vector.tensor_copy(gradient_2[:], gradient_pass(2, slice(0, N), 7))
-        nc.vector.tensor_copy(windows[2][:].indirect(offsets[:]), gradient_2[:])
-        store(2)
+        def vector_scatter(e, gradient):
+            nc.vector.tensor_copy(windows[e][:].indirect(listed(SECOND)), gradient)
+            store(e)
 
-        gradient_3 = keep.tile([P, N], F32, name="gradient_3")
-        for h in range(2):
-            nc.scalar.copy(gradient_3[:, halves[h]], gradient_pass(3, halves[h], (0, 2)[h]))
-        for slots in halves:
-            scalar_scatter(3, slots, gradient_3[:, slots])
-        store(3)
+        vector_scatter(0, late_halves[0][:])
+        scalar_scatter(1, FIRST, gradient_1[:, FIRST])
+        early_halves = [keep.tile([P, HALF], F32, name="early_half%d" % e) for e in (2, 3)]
+        for e in (2, 3):
+            nc.scalar.copy(early_halves[e - 2][:], gradient_pass(e, FIRST, (7, 2)[e - 2]))
+        nc.vector.tensor_copy(late_halves[2][:], gradient_pass(2, SECOND, 0))
+        vector_scatter(1, gradient_1[:, SECOND])
+        for e in (2, 3):
+            scalar_scatter(e, FIRST, early_halves[e - 2][:])
+        nc.vector.tensor_copy(late_halves[3][:], gradient_pass(3, SECOND, 3))
+        for e in (2, 3):
+            vector_scatter(e, late_halves[e][:])

@@ -16,31 +16,35 @@ E4M3X4 = mybir.dt.float8_e4m3fn_x4
 E5M2X4 = mybir.dt.float8_e5m2_x4
 COPY = mybir.ActivationFunctionType.Copy
 MULT = mybir.AluOpType.mult
+ADD = mybir.AluOpType.add
 SUBTRACT = mybir.AluOpType.subtract
 
 P = 128
 PACK = 4
 BAND = 16
 HALF = N // 2
+QUARTER = N // 4
 FIRST, SECOND = slice(0, HALF), slice(HALF, N)
 
 TARGETS_AT = 0
 X_GROUPED_WORD = 3 * HALF // 2
-X_GROUPED_STEP = 7 * HALF // 2
-FIRST_SCORES_AT = 7
-G_AT = 15
-XM_REST_AT = 8
-WORK_CELLS = 19
+X_GROUPED_STEP = 4 * HALF
+FIRST_SCORES_AT = 8
+XM_LAST_WORD = 19 * HALF // 2
+G_AT = 16
+WORK_CELLS = 20
 
 
 def tile_attend_gsq_w_kb_kernel(tc, xT, wT, y, wt, kb, xm, offs, out):
     nc = tc.nc
     halves = [FIRST, SECOND]
+    quarters = [slice(q * QUARTER, (q + 1) * QUARTER) for q in range(4)]
 
     with ExitStack() as ctx:
         keep = ctx.enter_context(tc.tile_pool(name="keep", bufs=1))
         shared = ctx.enter_context(tc.tile_pool(name="shared", bufs=1))
         cleared = ctx.enter_context(tc.tile_pool(name="cleared", bufs=1))
+        reused = ctx.enter_context(tc.tile_pool(name="reused", bufs=1))
         late = ctx.enter_context(tc.tile_pool(name="late", bufs=1))
         psum = ctx.enter_context(tc.psum_pool(name="psum", bufs=1))
 
@@ -60,7 +64,8 @@ def tile_attend_gsq_w_kb_kernel(tc, xT, wT, y, wt, kb, xm, offs, out):
         nc.sync.dma_start(kb_columns[:], kb[0].rearrange("(p c) -> p c", p=P))
 
         w_planes = wT.rearrange("(p t) c -> p t c", t=PACK)
-        w_raw = [keep.tile([P, T], F32, name="w_raw%d" % t) for t in range(PACK)]
+        w_raw = [keep.tile([P, T], F32, name="w_raw%d" % t) for t in range(PACK - 1)]
+        w_raw.append(reused.tile([P, T], F32, name="w_raw3", offset=0, align_bytes=64))
         nc.sync.dma_start(w_raw[0][:], w_planes[:, 0, :])
         offsets = keep.tile([P, N // BAND], U16, name="offsets")
         nc.sync.dma_start(offsets[:], offs)
@@ -69,7 +74,7 @@ def tile_attend_gsq_w_kb_kernel(tc, xT, wT, y, wt, kb, xm, offs, out):
         for t in range(1, PACK):
             nc.sync.dma_start(w_raw[t][:], w_planes[:, t, :])
 
-        work = shared.tile([P, WORK_CELLS * HALF], F32, name="work", offset=0, align_bytes=64)
+        work = reused.tile([P, WORK_CELLS * HALF], F32, name="work", offset=0, align_bytes=64)
 
         def cells(start, count):
             return work[:, start * HALF : (start + count) * HALF]
@@ -78,11 +83,15 @@ def tile_attend_gsq_w_kb_kernel(tc, xT, wT, y, wt, kb, xm, offs, out):
             return words.bitcast(BF16).rearrange("p (c t) -> p c t", t=PACK)
 
         targets = cells(TARGETS_AT, 2 * PACK).rearrange("p (s h c) -> p h s c", h=2, s=PACK)
+        target_planes = cells(TARGETS_AT, 2 * PACK).rearrange("p (s n) -> p s n", s=PACK)
         scores = cells(FIRST_SCORES_AT, 2 * PACK).rearrange("p (h s c) -> p h s c", h=2, s=PACK)
         x_planes = xT[0].rearrange("(p t) r -> p t r", t=PACK)
-        x_pairs = [keep.tile([P, 2, R], F32, name="x_pair%d" % u) for u in range(2)]
+        x_pairs = [
+            keep.tile([P, 2, R], F32, name="x_pair0")[:],
+            late.tile([P, 2, R], F32, name="x_pair1", offset=5120, align_bytes=64)[:],
+        ]
         for u in range(2):
-            nc.sync.dma_start(x_pairs[u][:], x_planes[:, 2 * u : 2 * u + 2, :])
+            nc.sync.dma_start(x_pairs[u], x_planes[:, 2 * u : 2 * u + 2, :])
 
         y_planes = y[0].rearrange("(p t) n -> p t n", t=PACK)
         y_pairs = [keep.tile([P, 2, N], F32, name="y_pair%d" % u) for u in range(2)]
@@ -118,38 +127,29 @@ def tile_attend_gsq_w_kb_kernel(tc, xT, wT, y, wt, kb, xm, offs, out):
 
         kb_listed = keep.tile([P, N], F32, name="kb_listed", align_bytes=64)
         nc.vector.tensor_copy(kb_listed[:], kb_window[:].indirect(offsets[:]))
-        kb_weighted = keep.tile([P, PACK, 2, HALF], F32, name="kb_weighted")
+        kb_weighted = [keep.tile([P, N], F32, name="kb_weighted%d" % t)[:] for t in range(PACK)]
         for t in range(PACK):
-            nc.scalar.activation(
-                kb_weighted[:, t].rearrange("p h c -> p (h c)"), kb_listed[:], COPY, scale=row_weight[:, t : t + 1]
-            )
+            nc.scalar.activation(kb_weighted[t], kb_listed[:], COPY, scale=row_weight[:, t : t + 1])
 
-        x_spaced = work[:, X_GROUPED_WORD : X_GROUPED_WORD + 2 * X_GROUPED_STEP].bitcast(BF16)
-        x_spaced = x_spaced.rearrange("p (v z) -> p v z", v=2)
-        w_listed = [x_spaced[:, h, 0 : 3 * HALF].rearrange("p (r c) -> p r c", r=3) for h in range(2)]
         w_grouped = [
-            keep.tile([P, HALF, PACK], BF16, name="w_grouped%d" % h, align_bytes=64) for h in range(2)
+            shared.tile([P, HALF, PACK], BF16, name="w_grouped0", offset=0, align_bytes=64),
+            keep.tile([P, HALF, PACK], BF16, name="w_grouped1", align_bytes=64),
         ]
+        w_listed = shared.tile([P, 3, HALF], BF16, name="w_listed", offset=2048, align_bytes=64)
         w_row = (1, 2, 0, 1)
 
-        def group_pair(copy, u, h):
-            pair = w_listed[h][:, w_row[2 * u] : w_row[2 * u] + 2]
-            copy(w_grouped[h][:, :, 2 * u : 2 * u + 2], pair.rearrange("p t c -> p c t"))
+        def group_pair(u):
+            pair = w_listed[:, w_row[2 * u] : w_row[2 * u] + 2]
+            nc.scalar.copy(w_grouped[1][:, :, 2 * u : 2 * u + 2], pair.rearrange("p t c -> p c t"))
 
-        def gather(t, h):
-            nc.vector.tensor_copy(w_listed[h][:, w_row[t]], w_raw[t][:].indirect(listed(halves[h])))
-
-        for t in range(2):
-            for h in range(2):
-                gather(t, h)
-        for h in range(2):
-            group_pair(nc.scalar.copy, 0, h)
-        for h in range(2):
-            gather(2, h)
-        gather(3, 0)
-        nc.scalar.activation(w_listed[1][:, w_row[3]], w_raw[3][:].indirect(listed(SECOND)), COPY)
-        group_pair(nc.vector.tensor_copy, 1, 0)
-        group_pair(nc.scalar.copy, 1, 1)
+        for t in range(PACK):
+            nc.vector.tensor_copy(w_grouped[0][:, :, t], w_raw[t][:].indirect(listed(FIRST)))
+            if t < PACK - 1:
+                nc.vector.tensor_copy(w_listed[:, w_row[t]], w_raw[t][:].indirect(listed(SECOND)))
+            else:
+                nc.scalar.activation(w_listed[:, w_row[t]], w_raw[t][:].indirect(listed(SECOND)), COPY)
+            if t % 2 == 1:
+                group_pair(t // 2)
         w_codes = [
             late.tile([P, HALF], U32, name="w_codes0", offset=0, align_bytes=64),
             keep.tile([P, HALF], U32, name="w_codes1", align_bytes=64),
@@ -157,24 +157,33 @@ def tile_attend_gsq_w_kb_kernel(tc, xT, wT, y, wt, kb, xm, offs, out):
         w_scales = keep.tile([P, N], U8, name="w_scales", align_bytes=64)
         quantize(w_codes[0][:], w_scales[:, FIRST], w_grouped[0][:], E4M3X4)
 
-        x_grouped = x_spaced[:, :, 0 : 2 * P * PACK].rearrange("p v (s m t) -> p v s m t", s=2, t=PACK)
-        for u in range(2):
-            rows = x_pairs[u][:].rearrange("p t (m v s) -> p v m t s", v=2, s=2)
-            for v, copy in enumerate((nc.vector.tensor_copy, nc.scalar.copy)):
-                copy(x_grouped[:, v, :, :, 2 * u : 2 * u + 2].rearrange("p s m t -> p m t s"), rows[:, v])
+        x_spaced = work[:, X_GROUPED_WORD : X_GROUPED_WORD + 2 * X_GROUPED_STEP].bitcast(BF16)
+        x_grouped = x_spaced.rearrange("p (v z) -> p v z", v=2)[:, :, 0 : 2 * P * PACK]
+        x_grouped = x_grouped.rearrange("p v (s m t) -> p v s m t", s=2, t=PACK)
+
+        def deal_x(copy, u, vs):
+            rows = x_pairs[u].rearrange("p t (m v s) -> p m t v s", v=2, s=2)
+            copy(x_grouped[:, vs, :, :, 2 * u : 2 * u + 2].rearrange("p v s m t -> p m t v s"), rows[:, :, :, vs])
+
+        deal_x(nc.vector.tensor_copy, 0, slice(0, 2))
+        deal_x(nc.vector.tensor_copy, 1, slice(0, 1))
+        deal_x(nc.scalar.copy, 1, slice(1, 2))
         quantize(w_codes[1][:], w_scales[:, SECOND], w_grouped[1][:], E4M3X4)
-        x_codes = keep.tile([P, R], U32, name="x_codes", align_bytes=64)
+        x_codes = [
+            late.tile([P, 2 * P], U32, name="x_codes0", offset=5120, align_bytes=64),
+            keep.tile([P, 2 * P], U32, name="x_codes1", align_bytes=64),
+        ]
         x_scales = keep.tile([P, R], U8, name="x_scales", align_bytes=64)
         for v in range(2):
             cols = slice(2 * P * v, 2 * P * (v + 1))
-            quantize(x_codes[:, cols], x_scales[:, cols], x_grouped[:, v].rearrange("p s m t -> p (s m) t"), E4M3X4)
+            quantize(x_codes[v][:], x_scales[:, cols], x_grouped[:, v].rearrange("p s m t -> p (s m) t"), E4M3X4)
 
         def weigh_scores(h, s):
             rows = slice(s * P, (s + 1) * P)
-            bank = psum.tile([P, HALF], F32, name="score_bank", tag="bank%d" % ((4 + 4 * h + s) % 8))
+            bank = psum.tile([P, HALF], F32, name="score_bank", tag="bank%d" % (4 + s))
             nc.tensor.matmul_mx(
                 out=bank[:],
-                lhsT=x_codes[:, rows].bitcast(E4M3X4),
+                lhsT=x_codes[s // 2][:, s % 2 * P : (s % 2 + 1) * P].bitcast(E4M3X4),
                 lhsT_scale=x_scales[:, rows],
                 rhs=w_codes[h][:].bitcast(E4M3X4),
                 rhs_scale=w_scales[:, halves[h]],
@@ -183,18 +192,16 @@ def tile_attend_gsq_w_kb_kernel(tc, xT, wT, y, wt, kb, xm, offs, out):
             )
             nc.scalar.activation(scores[:, h, s], bank[:], COPY, scale=row_weight[:, s : s + 1])
 
-        def weigh_target(s, hs):
-            y_plane = y_pairs[s // 2][:, s % 2, :].rearrange("p (h c) -> p h c", h=2)
+        def weigh_target(s, slots):
             nc.vector.scalar_tensor_tensor(
-                targets[:, hs, s],
-                y_plane[:, hs],
+                target_planes[:, s, slots],
+                y_pairs[s // 2][:, s % 2, slots],
                 row_weight[:, s : s + 1],
-                kb_weighted[:, s, hs],
+                kb_weighted[s][:, slots],
                 MULT,
                 SUBTRACT,
             )
 
-        first, second, both = slice(0, 1), slice(1, 2), slice(0, 2)
         xm_first = late.tile([P, P, PACK], BF16, name="xm_first", offset=0, align_bytes=64)
         for s in range(PACK):
             weigh_scores(0, s)
@@ -202,11 +209,11 @@ def tile_attend_gsq_w_kb_kernel(tc, xT, wT, y, wt, kb, xm, offs, out):
             if s == 2:
                 nc.scalar.copy(*by_fours(xm_first[:], xm_halves[0][:, :, 0:P]))
             weigh_scores(1, s)
-        weigh_target(0, both)
-        weigh_target(1, first)
-        weigh_target(2, both)
-        weigh_target(3, first)
-        weigh_target(1, second)
+        weigh_target(0, slice(0, N))
+        weigh_target(1, slice(0, N))
+        weigh_target(2, FIRST)
+        weigh_target(3, quarters[0])
+        weigh_target(3, quarters[1])
 
         g_codes = keep.tile([P, N], U32, name="g_codes", align_bytes=64)
         g_scales = keep.tile([P, N], U8, name="g_scales", align_bytes=64)
@@ -214,13 +221,14 @@ def tile_attend_gsq_w_kb_kernel(tc, xT, wT, y, wt, kb, xm, offs, out):
         xm_codes = keep.tile([P, D], U32, name="xm_codes", align_bytes=64)
         g_grouped = grouped_view(cells(G_AT, 4))
         xm_second = grouped_view(scores[:, 0, 1])
-        xm_rest = grouped_view(cells(XM_REST_AT, 2))
+        xm_last = grouped_view(work[:, XM_LAST_WORD : XM_LAST_WORD + HALF])
 
-        def form_g(h):
+        def form_g(q):
+            part = slice(q % 2 * QUARTER, (q % 2 + 1) * QUARTER)
             nc.vector.tensor_tensor(
-                g_grouped[:, halves[h], :].rearrange("p (c i) s -> p c s i", i=4),
-                scores[:, h].rearrange("p s (c i) -> p c s i", i=4),
-                targets[:, h].rearrange("p s (c i) -> p c s i", i=4),
+                g_grouped[:, quarters[q], :].rearrange("p (c i) s -> p c s i", i=4),
+                scores[:, q // 2, :, part].rearrange("p s (c i) -> p c s i", i=4),
+                targets[:, q // 2, :, part].rearrange("p s (c i) -> p c s i", i=4),
                 SUBTRACT,
             )
 
@@ -251,39 +259,49 @@ def tile_attend_gsq_w_kb_kernel(tc, xT, wT, y, wt, kb, xm, offs, out):
             nc.sync.dma_start(out[e * P : (e + 1) * P, :], windows[e][:])
 
         form_g(0)
+        form_g(1)
+        quantize_g(quarters[0])
         quantize_xm(slice(0, P), xm_first[:])
-        weigh_target(3, second)
-        quantize_g(FIRST)
+        quantize_g(quarters[1])
         nc.scalar.copy(*by_fours(xm_second, xm_halves[0][:, :, P:]))
         gradient_a = keep.tile([P, HALF], F32, name="gradient_a")
-        nc.scalar.copy(gradient_a[:], gradient_pass(0, FIRST, 4))
+        nc.scalar.copy(gradient_a[:], gradient_pass(0, FIRST, 3))
         scalar_scatter(0, FIRST, gradient_a[:])
 
-        form_g(1)
+        weigh_target(2, SECOND)
+        weigh_target(3, quarters[2])
+        weigh_target(3, quarters[3])
+        form_g(2)
+        form_g(3)
+        quantize_g(quarters[2])
         quantize_xm(slice(P, 2 * P), xm_second)
-        quantize_g(SECOND)
-        nc.vector.tensor_copy(*by_fours(xm_rest, xm_halves[1][:]))
+        quantize_g(quarters[3])
+        nc.vector.tensor_copy(*by_fours(xm_second, xm_halves[1][:, :, 0:P]))
 
-        late_halves = [keep.tile([P, HALF], F32, name="late_half%d" % e) for e in range(PACK)]
-        nc.vector.tensor_copy(late_halves[0][:], gradient_pass(0, SECOND, 5))
-        gradient_1 = late.tile([P, N], F32, name="gradient_1", offset=1024, align_bytes=64)
+        gradient_b = keep.tile([P, HALF], F32, name="gradient_b")
+        for u in range(2):
+            part = slice(u * QUARTER, (u + 1) * QUARTER)
+            nc.vector.tensor_copy(gradient_b[:, part], gradient_pass(0, quarters[2 + u], (2, 7)[u]))
+        quantize_xm(slice(2 * P, 3 * P), xm_second)
+        nc.gpsimd.tensor_scalar(*by_fours(xm_last, xm_halves[1][:, :, P:]), 1.0, 0.0, MULT, ADD)
+        gradient_1 = [keep.tile([P, HALF], F32, name="gradient_1_%d" % h)[:] for h in range(2)]
         for h in range(2):
-            nc.scalar.copy(gradient_1[:, halves[h]], gradient_pass(1, halves[h], (6, 1)[h]))
-        quantize_xm(slice(2 * P, D), xm_rest)
+            nc.scalar.copy(gradient_1[h], gradient_pass(1, halves[h], (0, 1)[h]))
+        nc.vector.tensor_copy(windows[0][:].indirect(listed(SECOND)), gradient_b[:])
+        store(0)
+        for h in range(2):
+            scalar_scatter(1, halves[h], gradient_1[h])
+        store(1)
 
-        def vector_scatter(e, gradient):
-            nc.vector.tensor_copy(windows[e][:].indirect(listed(SECOND)), gradient)
-            store(e)
+        gradient_2 = keep.tile([P, N], F32, name="gradient_2")
+        nc.vector.tensor_copy(gradient_2[:], gradient_pass(2, slice(0, N), 4))
+        quantize_xm(slice(3 * P, D), xm_last)
+        nc.vector.tensor_copy(windows[2][:].indirect(offsets[:]), gradient_2[:])
+        store(2)
 
-        vector_scatter(0, late_halves[0][:])
-        scalar_scatter(1, FIRST, gradient_1[:, FIRST])
-        early_halves = [keep.tile([P, HALF], F32, name="early_half%d" % e) for e in (2, 3)]
-        for e in (2, 3):
-            nc.scalar.copy(early_halves[e - 2][:], gradient_pass(e, FIRST, (7, 2)[e - 2]))
-        nc.vector.tensor_copy(late_halves[2][:], gradient_pass(2, SECOND, 0))
-        vector_scatter(1, gradient_1[:, SECOND])
-        for e in (2, 3):
-            scalar_scatter(e, FIRST, early_halves[e - 2][:])
-        nc.vector.tensor_copy(late_halves[3][:], gradient_pass(3, SECOND, 3))
-        for e in (2, 3):
-            vector_scatter(e, late_halves[e][:])
+        gradient_3 = keep.tile([P, N], F32, name="gradient_3")
+        for h in range(2):
+            nc.scalar.copy(gradient_3[:, halves[h]], gradient_pass(3, halves[h], (5, 6)[h]))
+        for slots in halves:
+            scalar_scatter(3, slots, gradient_3[:, slots])
+        store(3)

@@ -28,7 +28,7 @@ FIRST, SECOND = slice(0, HALF), slice(HALF, N)
 
 TARGETS_AT = 0
 X_GROUPED_WORD = 3 * HALF // 2
-X_GROUPED_STEP = 4 * HALF
+X_GROUPED_STEP = 2 * HALF
 FIRST_SCORES_AT = 8
 XM_LAST_WORD = 19 * HALF // 2
 G_AT = 16
@@ -70,7 +70,7 @@ def tile_attend_gsq_w_kb_kernel(tc, xT, wT, y, wt, kb, xm, offs, out):
         offsets = keep.tile([P, N // BAND], U16, name="offsets")
         nc.sync.dma_start(offsets[:], offs)
         row_weight = keep.tile([P, PACK], F32, name="row_weight")
-        nc.sync.dma_start(row_weight[:], wt[0].rearrange("(p t) o -> p (t o)", t=PACK))
+        nc.scalar.dma_start(row_weight[:], wt[0].rearrange("(p t) o -> p (t o)", t=PACK))
         for t in range(1, PACK):
             nc.sync.dma_start(w_raw[t][:], w_planes[:, t, :])
 
@@ -127,8 +127,8 @@ def tile_attend_gsq_w_kb_kernel(tc, xT, wT, y, wt, kb, xm, offs, out):
 
         kb_listed = keep.tile([P, N], F32, name="kb_listed", align_bytes=64)
         nc.vector.tensor_copy(kb_listed[:], kb_window[:].indirect(offsets[:]))
-        kb_weighted = [keep.tile([P, N], F32, name="kb_weighted%d" % t)[:] for t in range(PACK)]
-        for t in range(PACK):
+        kb_weighted = [keep.tile([P, N], F32, name="kb_weighted%d" % t)[:] for t in range(PACK - 1)]
+        for t in range(PACK - 1):
             nc.scalar.activation(kb_weighted[t], kb_listed[:], COPY, scale=row_weight[:, t : t + 1])
 
         w_grouped = [
@@ -138,13 +138,18 @@ def tile_attend_gsq_w_kb_kernel(tc, xT, wT, y, wt, kb, xm, offs, out):
         w_listed = shared.tile([P, 3, HALF], BF16, name="w_listed", offset=2048, align_bytes=64)
         w_row = (1, 2, 0, 1)
 
+        w_early = keep.tile([P, HALF], BF16, name="w_early", align_bytes=64)
+        nc.vector.tensor_copy(w_early[:], w_raw[0][:].indirect(listed(SECOND)))
+
         def group_pair(u):
             pair = w_listed[:, w_row[2 * u] : w_row[2 * u] + 2]
             nc.scalar.copy(w_grouped[1][:, :, 2 * u : 2 * u + 2], pair.rearrange("p t c -> p c t"))
 
         for t in range(PACK):
             nc.vector.tensor_copy(w_grouped[0][:, :, t], w_raw[t][:].indirect(listed(FIRST)))
-            if t < PACK - 1:
+            if t == 0:
+                nc.scalar.copy(w_listed[:, w_row[0]], w_early[:])
+            elif t < PACK - 1:
                 nc.vector.tensor_copy(w_listed[:, w_row[t]], w_raw[t][:].indirect(listed(SECOND)))
             else:
                 nc.scalar.activation(w_listed[:, w_row[t]], w_raw[t][:].indirect(listed(SECOND)), COPY)
@@ -168,6 +173,8 @@ def tile_attend_gsq_w_kb_kernel(tc, xT, wT, y, wt, kb, xm, offs, out):
         deal_x(nc.vector.tensor_copy, 0, slice(0, 2))
         deal_x(nc.vector.tensor_copy, 1, slice(0, 1))
         deal_x(nc.scalar.copy, 1, slice(1, 2))
+        kb_weighted.append(late.tile([P, N], F32, name="kb_weighted3", offset=6144, align_bytes=64)[:])
+        nc.scalar.activation(kb_weighted[3], kb_listed[:], COPY, scale=row_weight[:, 3:4])
         quantize(w_codes[1][:], w_scales[:, SECOND], w_grouped[1][:], E4M3X4)
         x_codes = [
             late.tile([P, 2 * P], U32, name="x_codes0", offset=5120, align_bytes=64),

from contextlib import ExitStack

import concourse.mybir as mybir
from concourse.masks import make_identity

D, R, N, T = 512, 512, 512, 2048
FLOPS = 2 * (2 * D * R * N)

F32 = mybir.dt.float32
BF16 = mybir.dt.bfloat16
I32 = mybir.dt.int32
U32 = mybir.dt.uint32
U16 = mybir.dt.uint16
U8 = mybir.dt.uint8
E4M3X4 = mybir.dt.float8_e4m3fn_x4
E5M2X4 = mybir.dt.float8_e5m2_x4
COPY = mybir.ActivationFunctionType.Copy
MULT = mybir.AluOpType.mult
ADD = mybir.AluOpType.add
SUBTRACT = mybir.AluOpType.subtract

P = 128
PACK = 4
BAND = 16
HALF = N // 2
QUARTER = N // 4
FIRST, SECOND = slice(0, HALF), slice(HALF, N)

TARGETS_AT = 0
X_GROUPED_WORD = 3 * HALF // 2
X_GROUPED_STEP = 2 * HALF
FIRST_SCORES_AT = 8
XM_LAST_WORD = 19 * HALF // 2
G_AT = 16
WORK_CELLS = 20


def tile_attend_gsq_w_kb_kernel(tc, xT, wT, y, wt, kb, xm, offs, out):
    nc = tc.nc
    halves = [FIRST, SECOND]
    quarters = [slice(q * QUARTER, (q + 1) * QUARTER) for q in range(4)]

    with ExitStack() as ctx:
        keep = ctx.enter_context(tc.tile_pool(name="keep", bufs=1))
        shared = ctx.enter_context(tc.tile_pool(name="shared", bufs=1))
        cleared = ctx.enter_context(tc.tile_pool(name="cleared", bufs=1))
        reused = ctx.enter_context(tc.tile_pool(name="reused", bufs=1))
        late = ctx.enter_context(tc.tile_pool(name="late", bufs=1))
        psum = ctx.enter_context(tc.psum_pool(name="psum", bufs=1))

        def quantize(codes, scales, grouped, dtype):
            nc.vector.quantize_mx(out=codes.bitcast(dtype), scales=scales, in_=grouped.rearrange("p c t -> p (c t)"))

        def by_fours(grouped, planes):
            return (
                grouped.rearrange("p (c i) t -> p c t i", i=4),
                planes.rearrange("p t (c i) -> p c t i", i=4),
            )

        def listed(slots):
            return offsets[:, slots.start // BAND : slots.stop // BAND]

        kb_columns = keep.tile([P, T // P], F32, name="kb_columns")
        nc.sync.dma_start(kb_columns[:], kb[0].rearrange("(p c) -> p c", p=P))

        w_planes = wT.rearrange("(p t) c -> p t c", t=PACK)
        w_raw = [keep.tile([P, T], F32, name="w_raw%d" % t) for t in range(PACK - 1)]
        w_raw.append(reused.tile([P, T], F32, name="w_raw3", offset=0, align_bytes=64))
        nc.sync.dma_start(w_raw[0][:], w_planes[:, 0, :])
        offsets = keep.tile([P, N // BAND], U16, name="offsets")
        nc.sync.dma_start(offsets[:], offs)
        row_weight = keep.tile([P, PACK], F32, name="row_weight")
        nc.scalar.dma_start(row_weight[:], wt[0].rearrange("(p t) o -> p (t o)", t=PACK))
        for t in range(1, PACK):
            nc.sync.dma_start(w_raw[t][:], w_planes[:, t, :])

        work = reused.tile([P, WORK_CELLS * HALF], F32, name="work", offset=0, align_bytes=64)

        def cells(start, count):
            return work[:, start * HALF : (start + count) * HALF]

        def grouped_view(words):
            return words.bitcast(BF16).rearrange("p (c t) -> p c t", t=PACK)

        targets = cells(TARGETS_AT, 2 * PACK).rearrange("p (s h c) -> p h s c", h=2, s=PACK)
        target_planes = cells(TARGETS_AT, 2 * PACK).rearrange("p (s n) -> p s n", s=PACK)
        scores = cells(FIRST_SCORES_AT, 2 * PACK).rearrange("p (h s c) -> p h s c", h=2, s=PACK)
        x_planes = xT[0].rearrange("(p t) r -> p t r", t=PACK)
        x_pairs = [
            keep.tile([P, 2, R], F32, name="x_pair0")[:],
            late.tile([P, 2, R], F32, name="x_pair1", offset=5120, align_bytes=64)[:],
        ]
        for u in range(2):
            nc.sync.dma_start(x_pairs[u], x_planes[:, 2 * u : 2 * u + 2, :])

        y_planes = y[0].rearrange("(p t) n -> p t n", t=PACK)
        y_pairs = [keep.tile([P, 2, N], F32, name="y_pair%d" % u) for u in range(2)]
        for u in range(2):
            nc.sync.dma_start(y_pairs[u][:], y_planes[:, 2 * u : 2 * u + 2, :])

        xm_planes = xm[0].rearrange("(p t) d -> p t d", t=PACK)
        xm_halves = [
            keep.tile([P, PACK, D // 2], F32, name="xm_half0"),
            late.tile([P, PACK, D // 2], F32, name="xm_half1", offset=1024, align_bytes=64),
        ]
        for v in range(2):
            nc.sync.dma_start(xm_halves[v][:], xm_planes[:, :, v * (D // 2) : (v + 1) * (D // 2)])

        identity = cleared.tile([P, P], F32, name="identity", offset=4 * T - 256)
        make_identity(nc, identity[:])
        windows = [keep.tile([P, T], F32, name="window%d" % w) for w in range(2)]
        for window in windows:
            nc.vector.memset(window[:].bitcast(I32), 0)
        kb_window = shared.tile([P, T], F32, name="kb_window", offset=0, align_bytes=64)
        kb_items = kb_window[:].rearrange("p (n c) -> p n c", n=P)
        turns_per_bank = N // P
        for c0 in range(0, T // P, turns_per_bank):
            spread = psum.tile([P, turns_per_bank, P], F32, name="spread", tag="bank%d" % (c0 // turns_per_bank))
            for c in range(turns_per_bank):
                column = kb_columns[:, c0 + c : c0 + c + 1]
                nc.tensor.transpose(spread[:, c, :], column.to_broadcast([P, P]), identity[:])
            nc.scalar.copy(kb_items[:, :, c0 : c0 + turns_per_bank], spread[:].rearrange("p c n -> p n c"))

        for w in range(2):
            windows.append(cleared.tile([P, T], F32, name="window%d" % (2 + w), offset=4 * T * w))
            nc.gpsimd.memset(windows[-1][:].bitcast(I32), 0)

        kb_listed = keep.tile([P, N], F32, name="kb_listed", align_bytes=64)
        nc.vector.tensor_copy(kb_listed[:], kb_window[:].indirect(offsets[:]))
        kb_weighted = [keep.tile([P, N], F32, name="kb_weighted%d" % t)[:] for t in range(PACK - 1)]
        for t in range(PACK - 1):
            nc.scalar.activation(kb_weighted[t], kb_listed[:], COPY, scale=row_weight[:, t : t + 1])

        w_grouped = [
            shared.tile([P, HALF, PACK], BF16, name="w_grouped0", offset=0, align_bytes=64),
            keep.tile([P, HALF, PACK], BF16, name="w_grouped1", align_bytes=64),
        ]
        w_listed = shared.tile([P, 3, HALF], BF16, name="w_listed", offset=2048, align_bytes=64)
        w_row = (1, 2, 0, 1)

        w_early = keep.tile([P, HALF], BF16, name="w_early", align_bytes=64)
        nc.vector.tensor_copy(w_early[:], w_raw[0][:].indirect(listed(SECOND)))

        def group_pair(u):
            pair = w_listed[:, w_row[2 * u] : w_row[2 * u] + 2]
            nc.scalar.copy(w_grouped[1][:, :, 2 * u : 2 * u + 2], pair.rearrange("p t c -> p c t"))

        for t in range(PACK):
            nc.vector.tensor_copy(w_grouped[0][:, :, t], w_raw[t][:].indirect(listed(FIRST)))
            if t == 0:
                nc.scalar.copy(w_listed[:, w_row[0]], w_early[:])
            elif t < PACK - 1:
                nc.vector.tensor_copy(w_listed[:, w_row[t]], w_raw[t][:].indirect(listed(SECOND)))
            else:
                nc.scalar.activation(w_listed[:, w_row[t]], w_raw[t][:].indirect(listed(SECOND)), COPY)
            if t % 2 == 1:
                group_pair(t // 2)
        w_codes = [
            late.tile([P, HALF], U32, name="w_codes0", offset=0, align_bytes=64),
            keep.tile([P, HALF], U32, name="w_codes1", align_bytes=64),
        ]
        w_scales = keep.tile([P, N], U8, name="w_scales", align_bytes=64)
        quantize(w_codes[0][:], w_scales[:, FIRST], w_grouped[0][:], E4M3X4)

        x_spaced = work[:, X_GROUPED_WORD : X_GROUPED_WORD + 2 * X_GROUPED_STEP].bitcast(BF16)
        x_grouped = x_spaced.rearrange("p (v z) -> p v z", v=2)[:, :, 0 : 2 * P * PACK]
        x_grouped = x_grouped.rearrange("p v (s m t) -> p v s m t", s=2, t=PACK)

        def deal_x(copy, u, vs):
            rows = x_pairs[u].rearrange("p t (m v s) -> p m t v s", v=2, s=2)
            copy(x_grouped[:, vs, :, :, 2 * u : 2 * u + 2].rearrange("p v s m t -> p m t v s"), rows[:, :, :, vs])

        deal_x(nc.vector.tensor_copy, 0, slice(0, 2))
        deal_x(nc.vector.tensor_copy, 1, slice(0, 1))
        deal_x(nc.scalar.copy, 1, slice(1, 2))
        kb_weighted.append(late.tile([P, N], F32, name="kb_weighted3", offset=6144, align_bytes=64)[:])
        nc.scalar.activation(kb_weighted[3], kb_listed[:], COPY, scale=row_weight[:, 3:4])
        quantize(w_codes[1][:], w_scales[:, SECOND], w_grouped[1][:], E4M3X4)
        x_codes = [
            late.tile([P, 2 * P], U32, name="x_codes0", offset=5120, align_bytes=64),
            keep.tile([P, 2 * P], U32, name="x_codes1", align_bytes=64),
        ]
        x_scales = keep.tile([P, R], U8, name="x_scales", align_bytes=64)
        for v in range(2):
            cols = slice(2 * P * v, 2 * P * (v + 1))
            quantize(x_codes[v][:], x_scales[:, cols], x_grouped[:, v].rearrange("p s m t -> p (s m) t"), E4M3X4)

        def weigh_scores(h, s):
            rows = slice(s * P, (s + 1) * P)
            bank = psum.tile([P, HALF], F32, name="score_bank", tag="bank%d" % (4 + s))
            nc.tensor.matmul_mx(
                out=bank[:],
                lhsT=x_codes[s // 2][:, s % 2 * P : (s % 2 + 1) * P].bitcast(E4M3X4),
                lhsT_scale=x_scales[:, rows],
                rhs=w_codes[h][:].bitcast(E4M3X4),
                rhs_scale=w_scales[:, halves[h]],
                start=True,
                stop=True,
            )
            nc.scalar.activation(scores[:, h, s], bank[:], COPY, scale=row_weight[:, s : s + 1])

        def weigh_target(s, slots):
            nc.vector.scalar_tensor_tensor(
                target_planes[:, s, slots],
                y_pairs[s // 2][:, s % 2, slots],
                row_weight[:, s : s + 1],
                kb_weighted[s][:, slots],
                MULT,
                SUBTRACT,
            )

        xm_first = late.tile([P, P, PACK], BF16, name="xm_first", offset=0, align_bytes=64)
        for s in range(PACK):
            weigh_scores(0, s)
        for s in range(PACK):
            if s == 2:
                nc.scalar.copy(*by_fours(xm_first[:], xm_halves[0][:, :, 0:P]))
            weigh_scores(1, s)
        weigh_target(0, slice(0, N))
        weigh_target(1, slice(0, N))
        weigh_target(2, FIRST)
        weigh_target(3, quarters[0])
        weigh_target(3, quarters[1])

        g_codes = keep.tile([P, N], U32, name="g_codes", align_bytes=64)
        g_scales = keep.tile([P, N], U8, name="g_scales", align_bytes=64)
        xm_scales = keep.tile([P, D], U8, name="xm_scales", align_bytes=64)
        xm_codes = keep.tile([P, D], U32, name="xm_codes", align_bytes=64)
        g_grouped = grouped_view(cells(G_AT, 4))
        xm_second = grouped_view(scores[:, 0, 1])
        xm_last = grouped_view(work[:, XM_LAST_WORD : XM_LAST_WORD + HALF])

        def form_g(q):
            part = slice(q % 2 * QUARTER, (q % 2 + 1) * QUARTER)
            nc.vector.tensor_tensor(
                g_grouped[:, quarters[q], :].rearrange("p (c i) s -> p c s i", i=4),
                scores[:, q // 2, :, part].rearrange("p s (c i) -> p c s i", i=4),
                targets[:, q // 2, :, part].rearrange("p s (c i) -> p c s i", i=4),
                SUBTRACT,
            )

        def quantize_g(slots):
            quantize(g_codes[:, slots], g_scales[:, slots], g_grouped[:, slots], E5M2X4)

        def quantize_xm(feats, grouped):
            quantize(xm_codes[:, feats], xm_scales[:, feats], grouped, E4M3X4)

        def gradient_pass(e, slots, bank):
            feats = slice(e * P, (e + 1) * P)
            gradient_bank = psum.tile([P, slots.stop - slots.start], F32, name="gradient_bank", tag="bank%d" % bank)
            nc.tensor.matmul_mx(
                out=gradient_bank[:],
                lhsT=xm_codes[:, feats].bitcast(E4M3X4),
                lhsT_scale=xm_scales[:, feats],
                rhs=g_codes[:, slots].bitcast(E5M2X4),
                rhs_scale=g_scales[:, slots],
                start=True,
                stop=True,
            )
            return gradient_bank[:]

        def scalar_scatter(e, slots, gradient):
            nc.scalar.activation(windows[e][:].indirect(listed(slots)), gradient, COPY)

        def store(e):
            nc.sync.dma_start(out[e * P : (e + 1) * P, :], windows[e][:])

        form_g(0)
        form_g(1)
        quantize_g(quarters[0])
        quantize_xm(slice(0, P), xm_first[:])
        quantize_g(quarters[1])
        nc.scalar.copy(*by_fours(xm_second, xm_halves[0][:, :, P:]))
        gradient_a = keep.tile([P, HALF], F32, name="gradient_a")
        nc.scalar.copy(gradient_a[:], gradient_pass(0, FIRST, 3))
        scalar_scatter(0, FIRST, gradient_a[:])

        weigh_target(2, SECOND)
        weigh_target(3, quarters[2])
        weigh_target(3, quarters[3])
        form_g(2)
        form_g(3)
        quantize_g(quarters[2])
        quantize_xm(slice(P, 2 * P), xm_second)
        quantize_g(quarters[3])
        nc.vector.tensor_copy(*by_fours(xm_second, xm_halves[1][:, :, 0:P]))

        gradient_b = keep.tile([P, HALF], F32, name="gradient_b")
        for u in range(2):
            part = slice(u * QUARTER, (u + 1) * QUARTER)
            nc.vector.tensor_copy(gradient_b[:, part], gradient_pass(0, quarters[2 + u], (2, 7)[u]))
        quantize_xm(slice(2 * P, 3 * P), xm_second)
        nc.gpsimd.tensor_scalar(*by_fours(xm_last, xm_halves[1][:, :, P:]), 1.0, 0.0, MULT, ADD)
        gradient_1 = [keep.tile([P, HALF], F32, name="gradient_1_%d" % h)[:] for h in range(2)]
        for h in range(2):
            nc.scalar.copy(gradient_1[h], gradient_pass(1, halves[h], (0, 1)[h]))
        nc.vector.tensor_copy(windows[0][:].indirect(listed(SECOND)), gradient_b[:])
        store(0)
        for h in range(2):
            scalar_scatter(1, halves[h], gradient_1[h])
        store(1)

        gradient_2 = keep.tile([P, N], F32, name="gradient_2")
        nc.vector.tensor_copy(gradient_2[:], gradient_pass(2, slice(0, N), 4))
        quantize_xm(slice(3 * P, D), xm_last)
        nc.vector.tensor_copy(windows[2][:].indirect(offsets[:]), gradient_2[:])
        store(2)

        gradient_3 = keep.tile([P, N], F32, name="gradient_3")
        for h in range(2):
            nc.scalar.copy(gradient_3[:, halves[h]], gradient_pass(3, halves[h], (5, 6)[h]))
        for slots in halves:
            scalar_scatter(3, slots, gradient_3[:, slots])
        store(3)
